import numpy as np
import ml_dtypes


def mxq(x, axis, fmt="e4m3"):
    dtype, down = {"e4m3": (ml_dtypes.float8_e4m3fn, 7), "e5m2": (ml_dtypes.float8_e5m2, 14)}[fmt]
    v = np.moveaxis(np.asarray(x, np.float32).astype(ml_dtypes.bfloat16).astype(np.float64), axis, -1)
    blocks = v.reshape(v.shape[:-1] + (-1, 32))
    amax = np.abs(blocks).max(-1, keepdims=True)
    byte = np.maximum(np.where(amax > 0, np.frexp(amax)[1] - 1 + 127, 0) - down, 1)
    scale = np.exp2(byte - 127.0)
    codes = (blocks / scale).astype(np.float32).astype(dtype).astype(np.float64)
    return np.moveaxis((codes * scale).reshape(v.shape), -1, axis)


WIDE = False


def mx_kscale(k, group=512):
    if not WIDE:
        return np.ones(k)
    levels = np.array([18, -18])
    if group != 512:
        return np.exp2(np.random.permutation(np.resize(levels, k // group))).repeat(group)
    if k % 512:
        return np.exp2(np.random.permutation(np.resize(levels, k // 32))).repeat(32)
    a = np.empty((k // 512, 16))
    for p in range(k // 512):
        a[p, :8] = np.random.permutation(np.resize(levels, 8))
        for g in range(8):
            far = levels[np.abs(levels - a[p, g]) >= 10]
            a[p, g + 8] = far[np.random.randint(len(far))]
    return np.exp2(a.ravel()).repeat(32)


def f64(x):
    return np.asarray(x).astype(np.float64)


H, D, N = 4, 128, 1024


def setup_inputs():
    n = np.random.standard_normal
    s = mx_kscale(D, 0)[:, None]
    S = n((H, D, 128)) / np.sqrt(D)
    return {
        "q": n((H, D, N)).astype(np.float32),
        "qa": (np.random.uniform(0.5, 2.0, (D, 1)) * s).astype(np.float32),
        "S": (S / s).astype(np.float32),
        "og": n((H, N, 128)).astype(np.float32),
    }


def reference(q, qa, S, og):
    fq = (np.maximum(f64(q), 0.0) + 0.125) * f64(qa)
    y = mxq(fq, 1, "e4m3").transpose(0, 2, 1) @ mxq(f64(S), 1, "e4m3")
    y = y / (1.0 + np.exp(-f64(og)))
    return y

@@ -1,0 +1,133 @@
+from contextlib import ExitStack
+
+import concourse.mybir as mybir
+
+H, D, N, E = 4, 128, 1024, 128
+FLOPS = 2 * H * N * D * E
+
+F32 = mybir.dt.float32
+BF16 = mybir.dt.bfloat16
+U32 = mybir.dt.uint32
+U8 = mybir.dt.uint8
+FP8X4 = mybir.dt.float8_e4m3fn_x4
+ACT = mybir.ActivationFunctionType
+ALU = mybir.AluOpType
+
+P = 128
+PACK = 4
+ROWS = D // PACK
+T = 8
+U = 2
+TU = T // U
+Q_CHUNKS = [128,128,256,256,256]
+HALF = P // 2
+
+
+def tile_rows_read_relu1_gate_kernel(tc, q, qa, S, og, out):
+    nc = tc.nc
+    q_v = q.rearrange("h (p j) n -> (h p) j n", j=PACK)
+    s_v = S.rearrange("h (p j) e -> (h p) j e", j=PACK)
+    qa_v = qa.rearrange("(p j) o -> p (j o)", j=PACK)
+
+    with ExitStack() as ctx:
+        sb = ctx.enter_context(tc.tile_pool(name="sb", bufs=1))
+        ps = ctx.enter_context(tc.psum_pool(name="ps", bufs=1))
+        ctx.enter_context(tc.manual_schedule())
+
+        weight = sb.tile([P, PACK], F32, name="weight")
+        for h in range(H):
+            nc.scalar.dma_start(out=weight[ROWS * h : ROWS * (h + 1), :], in_=qa_v)
+        warm_in = sb.tile([P, 1], F32, name="warm_in")
+        warm_out = sb.tile([P, 1], F32, name="warm_out")
+        nc.vector.memset(warm_in[:], 0.0)
+        nc.scalar.activation(out=warm_out[:], in_=warm_in[:], func=ACT.Sigmoid)
+
+        mc_max = max(Q_CHUNKS) // T
+        weight_run = sb.tile([P, mc_max, PACK], F32, name="weight_run")
+        nc.vector.tensor_copy(out=weight_run[:], in_=weight[:].unsqueeze(1).to_broadcast([P, mc_max, PACK]))
+
+        q_raw = []
+        n0 = 0
+        for c, width in enumerate(Q_CHUNKS):
+            raw = sb.tile([P, PACK, width], F32, name="q_raw%d" % c)
+            nc.sync.dma_start(out=raw[:], in_=q_v[:, :, n0 : n0 + width])
+            q_raw.append(raw)
+            n0 += width
+        s_raw = sb.tile([P, PACK, E], F32, name="s_raw")
+        nc.sync.dma_start(out=s_raw[:], in_=s_v)
+        gate = []
+        for h in range(H):
+            g = sb.tile([P, T * E], F32, name="gate%d" % h)
+            nc.sync.dma_start(out=g[:], in_=og[h].rearrange("(m t) e -> m (t e)", t=T))
+            gate.append(g)
+
+        fq = sb.tile([P, T, P, PACK], BF16, name="fq", align_bytes=64)
+        q_codes = sb.tile([P, T, P], U32, name="q_codes", align_bytes=64)
+        q_scales = sb.tile([P, T, P], U8, name="q_scales", align_bytes=64)
+
+        def quantize_q(t, half):
+            cols = slice(HALF * half, HALF * (half + 1))
+            nc.vector.quantize_mx(
+                out=q_codes[:, t, cols].bitcast(FP8X4),
+                scales=q_scales[:, t, cols],
+                in_=fq[:, t, cols, :].rearrange("p m j -> p (m j)"),
+            )
+
+        m0 = 0
+        for c, width in enumerate(Q_CHUNKS):
+            mc = width // T
+            src = q_raw[c][:].rearrange("p j (m u i) -> p u m j i", u=U, i=TU)
+            for u in range(U):
+                relu = sb.tile([P, TU, mc, PACK], F32, name="relu%d_%d" % (c, u))
+                nc.scalar.activation(out=relu[:].rearrange("p i m j -> p m j i"), in_=src[:, u], func=ACT.Relu)
+                nc.vector.scalar_tensor_tensor(
+                    out=fq[:, TU * u : TU * (u + 1), m0 : m0 + mc, :].rearrange("p i m j -> p i (m j)"),
+                    in0=relu[:].rearrange("p i m j -> p i (m j)"),
+                    scalar=0.125,
+                    in1=weight_run[:, :mc, :].rearrange("p m j -> p (m j)").unsqueeze(1).to_broadcast([P, TU, mc * PACK]),
+                    op0=ALU.add,
+                    op1=ALU.mult,
+                )
+            m0 += mc
+            if m0 == HALF:
+                for t in range(T):
+                    quantize_q(t, 0)
+
+        s_bf = sb.tile([P, E, PACK], BF16, name="s_bf", align_bytes=64)
+        s_codes = sb.tile([P, E], U32, name="s_codes", align_bytes=64)
+        s_scales = sb.tile([P, E], U8, name="s_scales", align_bytes=64)
+        nc.scalar.copy(out=s_bf[:], in_=s_raw[:].rearrange("p j e -> p e j"))
+
+        banks = {}
+        for h in range(H):
+            for u in range(U):
+                banks[h, u] = ps.tile([P, TU, E], F32, name="y%d_%d" % (h, u))
+
+        for t in range(TU):
+            quantize_q(t, 1)
+        nc.vector.quantize_mx(out=s_codes[:].bitcast(FP8X4), scales=s_scales[:], in_=s_bf[:].rearrange("p e j -> p (e j)"))
+        for t in range(TU, T):
+            quantize_q(t, 1)
+        for h in range(H):
+            for t in range(T):
+                rows = slice(ROWS * h, ROWS * (h + 1))
+                nc.tensor.matmul_mx(
+                    out=banks[h, t // TU][:, t % TU, :],
+                    lhsT=q_codes[rows, t, :].bitcast(FP8X4),
+                    lhsT_scale=q_scales[rows, t, :],
+                    rhs=s_codes[rows, :].bitcast(FP8X4),
+                    rhs_scale=s_scales[rows, :],
+                    start=True,
+                    stop=True,
+                )
+
+        for h in range(H):
+            res = sb.tile([P, T * E], F32, name="res%d" % h)
+            for u in range(U):
+                cols = slice(TU * E * u, TU * E * (u + 1))
+                sig = sb.tile([P, TU * E], F32, name="sig%d_%d" % (h, u))
+                nc.scalar.activation(out=sig[:], in_=gate[h][:, cols], func=ACT.Sigmoid)
+                nc.vector.tensor_tensor(
+                    out=res[:, cols], in0=banks[h, u][:].rearrange("p t e -> p (t e)"), in1=sig[:], op=ALU.mult
+                )
+            nc.sync.dma_start(out=out[h].rearrange("(m t) e -> m (t e)", t=T), in_=res[:])

@@ -16,11 +16,13 @@ ALU = mybir.AluOpType
 P = 128
 PACK = 4
 ROWS = D // PACK
-T = 8
-U = 2
-TU = T // U
-Q_CHUNKS = [128,128,256,256,256]
-HALF = P // 2
+T = 4
+GROUP = P * T
+GROUPS = N // GROUP
+PAIR = 2
+Q_CHUNKS = [256,256,256,256]
+PIECE = 128
+MP = PIECE // T
 
 
 def tile_rows_read_relu1_gate_kernel(tc, q, qa, S, og, out):
@@ -28,6 +30,8 @@ def tile_rows_read_relu1_gate_kernel(tc, q, qa, S, og, out):
     q_v = q.rearrange("h (p j) n -> (h p) j n", j=PACK)
     s_v = S.rearrange("h (p j) e -> (h p) j e", j=PACK)
     qa_v = qa.rearrange("(p j) o -> p (j o)", j=PACK)
+    og_v = og.rearrange("h (g m t) e -> g m h (t e)", g=GROUPS, t=T)
+    out_v = out.rearrange("h (g m t) e -> g m h (t e)", g=GROUPS, t=T)
 
     with ExitStack() as ctx:
         sb = ctx.enter_context(tc.tile_pool(name="sb", bufs=1))
@@ -35,99 +39,157 @@ def tile_rows_read_relu1_gate_kernel(tc, q, qa, S, og, out):
         ctx.enter_context(tc.manual_schedule())
 
         weight = sb.tile([P, PACK], F32, name="weight")
-        for h in range(H):
-            nc.scalar.dma_start(out=weight[ROWS * h : ROWS * (h + 1), :], in_=qa_v)
+
+        def load_weight(engine, h):
+            engine.dma_start(out=weight[ROWS * h : ROWS * (h + 1), :], in_=qa_v)
+
+        load_weight(nc.scalar, 0)
+        load_weight(nc.scalar, 1)
         warm_in = sb.tile([P, 1], F32, name="warm_in")
         warm_out = sb.tile([P, 1], F32, name="warm_out")
         nc.vector.memset(warm_in[:], 0.0)
         nc.scalar.activation(out=warm_out[:], in_=warm_in[:], func=ACT.Sigmoid)
 
-        mc_max = max(Q_CHUNKS) // T
-        weight_run = sb.tile([P, mc_max, PACK], F32, name="weight_run")
-        nc.vector.tensor_copy(out=weight_run[:], in_=weight[:].unsqueeze(1).to_broadcast([P, mc_max, PACK]))
-
-        q_raw = []
+        s_raw = sb.tile([P, PACK, E], F32, name="s_raw")
+        pieces = []
         n0 = 0
         for c, width in enumerate(Q_CHUNKS):
+            if c == 2:
+                nc.sync.dma_start(out=s_raw[:], in_=s_v)
             raw = sb.tile([P, PACK, width], F32, name="q_raw%d" % c)
             nc.sync.dma_start(out=raw[:], in_=q_v[:, :, n0 : n0 + width])
-            q_raw.append(raw)
+            if c == 0:
+                load_weight(nc.sync, 2)
+                load_weight(nc.sync, 3)
+            for o in range(0, width, PIECE):
+                pieces.append(raw[:, :, o : o + PIECE])
             n0 += width
-        s_raw = sb.tile([P, PACK, E], F32, name="s_raw")
-        nc.sync.dma_start(out=s_raw[:], in_=s_v)
-        gate = []
-        for h in range(H):
-            g = sb.tile([P, T * E], F32, name="gate%d" % h)
-            nc.sync.dma_start(out=g[:], in_=og[h].rearrange("(m t) e -> m (t e)", t=T))
-            gate.append(g)
-
-        fq = sb.tile([P, T, P, PACK], BF16, name="fq", align_bytes=64)
-        q_codes = sb.tile([P, T, P], U32, name="q_codes", align_bytes=64)
-        q_scales = sb.tile([P, T, P], U8, name="q_scales", align_bytes=64)
-
-        def quantize_q(t, half):
-            cols = slice(HALF * half, HALF * (half + 1))
-            nc.vector.quantize_mx(
-                out=q_codes[:, t, cols].bitcast(FP8X4),
-                scales=q_scales[:, t, cols],
-                in_=fq[:, t, cols, :].rearrange("p m j -> p (m j)"),
-            )
-
-        m0 = 0
-        for c, width in enumerate(Q_CHUNKS):
-            mc = width // T
-            src = q_raw[c][:].rearrange("p j (m u i) -> p u m j i", u=U, i=TU)
-            for u in range(U):
-                relu = sb.tile([P, TU, mc, PACK], F32, name="relu%d_%d" % (c, u))
-                nc.scalar.activation(out=relu[:].rearrange("p i m j -> p m j i"), in_=src[:, u], func=ACT.Relu)
-                nc.vector.scalar_tensor_tensor(
-                    out=fq[:, TU * u : TU * (u + 1), m0 : m0 + mc, :].rearrange("p i m j -> p i (m j)"),
-                    in0=relu[:].rearrange("p i m j -> p i (m j)"),
-                    scalar=0.125,
-                    in1=weight_run[:, :mc, :].rearrange("p m j -> p (m j)").unsqueeze(1).to_broadcast([P, TU, mc * PACK]),
-                    op0=ALU.add,
-                    op1=ALU.mult,
-                )
-            m0 += mc
-            if m0 == HALF:
-                for t in range(T):
-                    quantize_q(t, 0)
+        gate = {}
+        for g in range(GROUPS):
+            for k in range(H // PAIR):
+                gt = sb.tile([P, PAIR, T * E], F32, name="gate%d_%d" % (g, k))
+                nc.sync.dma_start(out=gt[:], in_=og_v[g, :, PAIR * k : PAIR * (k + 1), :])
+                gate[g, k] = gt
 
         s_bf = sb.tile([P, E, PACK], BF16, name="s_bf", align_bytes=64)
         s_codes = sb.tile([P, E], U32, name="s_codes", align_bytes=64)
         s_scales = sb.tile([P, E], U8, name="s_scales", align_bytes=64)
-        nc.scalar.copy(out=s_bf[:], in_=s_raw[:].rearrange("p j e -> p e j"))
 
-        banks = {}
-        for h in range(H):
-            for u in range(U):
-                banks[h, u] = ps.tile([P, TU, E], F32, name="y%d_%d" % (h, u))
+        def round_state():
+            nc.vector.tensor_copy(out=s_bf[:], in_=s_raw[:].rearrange("p j e -> p e j"))
 
-        for t in range(TU):
-            quantize_q(t, 1)
-        nc.vector.quantize_mx(out=s_codes[:].bitcast(FP8X4), scales=s_scales[:], in_=s_bf[:].rearrange("p e j -> p (e j)"))
-        for t in range(TU, T):
-            quantize_q(t, 1)
-        for h in range(H):
-            for t in range(T):
-                rows = slice(ROWS * h, ROWS * (h + 1))
-                nc.tensor.matmul_mx(
-                    out=banks[h, t // TU][:, t % TU, :],
-                    lhsT=q_codes[rows, t, :].bitcast(FP8X4),
-                    lhsT_scale=q_scales[rows, t, :],
-                    rhs=s_codes[rows, :].bitcast(FP8X4),
-                    rhs_scale=s_scales[rows, :],
-                    start=True,
-                    stop=True,
-                )
+        def quantize_state():
+            nc.vector.quantize_mx(out=s_codes[:].bitcast(FP8X4), scales=s_scales[:], in_=s_bf[:].rearrange("p e j -> p (e j)"))
 
-        for h in range(H):
-            res = sb.tile([P, T * E], F32, name="res%d" % h)
-            for u in range(U):
-                cols = slice(TU * E * u, TU * E * (u + 1))
-                sig = sb.tile([P, TU * E], F32, name="sig%d_%d" % (h, u))
-                nc.scalar.activation(out=sig[:], in_=gate[h][:, cols], func=ACT.Sigmoid)
-                nc.vector.tensor_tensor(
-                    out=res[:, cols], in0=banks[h, u][:].rearrange("p t e -> p (t e)"), in1=sig[:], op=ALU.mult
-                )
-            nc.sync.dma_start(out=out[h].rearrange("(m t) e -> m (t e)", t=T), in_=res[:])
+        fq, q_codes, q_scales, banks, res = {}, {}, {}, {}, {}
+        for g in range(GROUPS):
+            fq[g] = sb.tile([P, T, P, PACK], BF16, name="fq%d" % g, align_bytes=64)
+            q_codes[g] = sb.tile([P, T, P], U32, name="q_codes%d" % g, align_bytes=64)
+            q_scales[g] = sb.tile([P, T, P], U8, name="q_scales%d" % g, align_bytes=64)
+            for h in range(H):
+                banks[g, h] = ps.tile([P, T, E], F32, name="y%d_%d" % (g, h))
+            for k in range(H // PAIR):
+                res[g, k] = sb.tile([P, PAIR, T * E], F32, name="res%d_%d" % (g, k))
+
+        def feature_map(i):
+            g, m0 = divmod(i * MP, P)
+            relu = sb.tile([P, T, MP, PACK], F32, name="relu%d" % i)
+            nc.scalar.activation(
+                out=relu[:].rearrange("p t m j -> p m j t"),
+                in_=pieces[i].rearrange("p j (m t) -> p m j t", t=T),
+                func=ACT.Relu,
+            )
+            nc.vector.scalar_tensor_tensor(
+                out=fq[g][:, :, m0 : m0 + MP, :].rearrange("p t m j -> p t (m j)"),
+                in0=relu[:].rearrange("p t m j -> p t (m j)"),
+                scalar=0.125,
+                in1=weight[:].unsqueeze(1).to_broadcast([P, T * MP, PACK]),
+                op0=ALU.add,
+                op1=ALU.mult,
+            )
+
+        def multiply(g):
+            nc.vector.quantize_mx(
+                out=q_codes[g][:].rearrange("p t m -> p (t m)").bitcast(FP8X4),
+                scales=q_scales[g][:].rearrange("p t m -> p (t m)"),
+                in_=fq[g][:].rearrange("p t m j -> p (t m j)"),
+            )
+            for k in range(H // PAIR):
+                for t in range(T):
+                    for h in range(PAIR * k, PAIR * (k + 1)):
+                        rows = slice(ROWS * h, ROWS * (h + 1))
+                        nc.tensor.matmul_mx(
+                            out=banks[g, h][:, t, :],
+                            lhsT=q_codes[g][rows, t, :].bitcast(FP8X4),
+                            lhsT_scale=q_scales[g][rows, t, :],
+                            rhs=s_codes[rows, :].bitcast(FP8X4),
+                            rhs_scale=s_scales[rows, :],
+                            start=True,
+                            stop=True,
+                        )
+
+        sig = {}
+
+        def sigmoid(g, h):
+            sig[g, h] = sb.tile([P, T * E], F32, name="sig%d_%d" % (g, h))
+            nc.scalar.activation(out=sig[g, h][:], in_=gate[g, h // PAIR][:, h % PAIR, :], func=ACT.Sigmoid)
+
+        def gate_vector(g, h, c0=0, c1=T * E):
+            nc.vector.tensor_tensor(
+                out=res[g, h // PAIR][:, h % PAIR, c0:c1],
+                in0=banks[g, h][:].rearrange("p t e -> p (t e)")[:, c0:c1],
+                in1=sig[g, h][:, c0:c1],
+                op=ALU.mult,
+            )
+
+        sums = {}
+
+        def copy_out(g, h):
+            sums[g, h] = sb.tile([P, T * E], F32, name="sums%d_%d" % (g, h))
+            nc.scalar.copy(out=sums[g, h][:], in_=banks[g, h][:].rearrange("p t e -> p (t e)"))
+
+        def gate_gpsimd(g, h):
+            nc.gpsimd.tensor_tensor(out=res[g, h // PAIR][:, h % PAIR, :], in0=sums[g, h][:], in1=sig[g, h][:], op=ALU.mult)
+
+        def store_pair(g, k):
+            nc.sync.dma_start(out=out_v[g, :, PAIR * k : PAIR * (k + 1), :], in_=res[g, k][:])
+
+        def store_head(g, h, c0=0, c1=T * E):
+            nc.sync.dma_start(out=out_v[g, :, h, c0:c1], in_=res[g, h // PAIR][:, h % PAIR, c0:c1])
+
+        feature_map(0)
+        feature_map(1)
+        round_state()
+        feature_map(2)
+        feature_map(3)
+        quantize_state()
+        multiply(0)
+        feature_map(4)
+        feature_map(5)
+        feature_map(6)
+        feature_map(7)
+        sigmoid(0, 0)
+        gate_vector(0, 0)
+        store_head(0, 0)
+        sigmoid(0, 1)
+        gate_vector(0, 1)
+        store_head(0, 1)
+        multiply(1)
+        sigmoid(0, 2)
+        gate_vector(0, 2)
+        store_head(0, 2)
+        sigmoid(0, 3)
+        gate_vector(0, 3)
+        store_head(0, 3)
+        sigmoid(1, 0)
+        gate_vector(1, 0)
+        store_head(1, 0)
+        sigmoid(1, 1)
+        gate_vector(1, 1)
+        store_head(1, 1)
+        sigmoid(1, 2)
+        gate_vector(1, 2)
+        store_head(1, 2)
+        sigmoid(1, 3)
+        gate_vector(1, 3)
+        store_head(1, 3)

@@ -20,9 +20,7 @@ T = 4
 GROUP = P * T
 GROUPS = N // GROUP
 PAIR = 2
-Q_CHUNKS = [256,256,256,256]
-PIECE = 128
-MP = PIECE // T
+CHUNK = 256
 
 
 def tile_rows_read_relu1_gate_kernel(tc, q, qa, S, og, out):
@@ -39,81 +37,82 @@ def tile_rows_read_relu1_gate_kernel(tc, q, qa, S, og, out):
         ctx.enter_context(tc.manual_schedule())
 
         weight = sb.tile([P, PACK], F32, name="weight")
-
-        def load_weight(engine, h):
-            engine.dma_start(out=weight[ROWS * h : ROWS * (h + 1), :], in_=qa_v)
-
-        load_weight(nc.scalar, 0)
-        load_weight(nc.scalar, 1)
-        warm_in = sb.tile([P, 1], F32, name="warm_in")
-        warm_out = sb.tile([P, 1], F32, name="warm_out")
-        nc.vector.memset(warm_in[:], 0.0)
-        nc.scalar.activation(out=warm_out[:], in_=warm_in[:], func=ACT.Sigmoid)
-
         s_raw = sb.tile([P, PACK, E], F32, name="s_raw")
-        pieces = []
-        n0 = 0
-        for c, width in enumerate(Q_CHUNKS):
-            if c == 2:
-                nc.sync.dma_start(out=s_raw[:], in_=s_v)
-            raw = sb.tile([P, PACK, width], F32, name="q_raw%d" % c)
-            nc.sync.dma_start(out=raw[:], in_=q_v[:, :, n0 : n0 + width])
-            if c == 0:
-                load_weight(nc.sync, 2)
-                load_weight(nc.sync, 3)
-            for o in range(0, width, PIECE):
-                pieces.append(raw[:, :, o : o + PIECE])
-            n0 += width
-        gate = {}
-        for g in range(GROUPS):
-            for k in range(H // PAIR):
-                gt = sb.tile([P, PAIR, T * E], F32, name="gate%d_%d" % (g, k))
-                nc.sync.dma_start(out=gt[:], in_=og_v[g, :, PAIR * k : PAIR * (k + 1), :])
-                gate[g, k] = gt
-
         s_bf = sb.tile([P, E, PACK], BF16, name="s_bf", align_bytes=64)
         s_codes = sb.tile([P, E], U32, name="s_codes", align_bytes=64)
         s_scales = sb.tile([P, E], U8, name="s_scales", align_bytes=64)
-
-        def round_state():
-            nc.vector.tensor_copy(out=s_bf[:], in_=s_raw[:].rearrange("p j e -> p e j"))
-
-        def quantize_state():
-            nc.vector.quantize_mx(out=s_codes[:].bitcast(FP8X4), scales=s_scales[:], in_=s_bf[:].rearrange("p e j -> p (e j)"))
-
-        fq, q_codes, q_scales, banks, res = {}, {}, {}, {}, {}
+        q_raw, gate, fq, q_codes, q_scales, banks, res, sig, relu = {}, {}, {}, {}, {}, {}, {}, {}, {}
         for g in range(GROUPS):
             fq[g] = sb.tile([P, T, P, PACK], BF16, name="fq%d" % g, align_bytes=64)
             q_codes[g] = sb.tile([P, T, P], U32, name="q_codes%d" % g, align_bytes=64)
             q_scales[g] = sb.tile([P, T, P], U8, name="q_scales%d" % g, align_bytes=64)
             for h in range(H):
                 banks[g, h] = ps.tile([P, T, E], F32, name="y%d_%d" % (g, h))
+                sig[g, h] = sb.tile([P, T * E], F32, name="sig%d_%d" % (g, h))
             for k in range(H // PAIR):
                 res[g, k] = sb.tile([P, PAIR, T * E], F32, name="res%d_%d" % (g, k))
 
-        def feature_map(i):
-            g, m0 = divmod(i * MP, P)
-            relu = sb.tile([P, T, MP, PACK], F32, name="relu%d" % i)
-            nc.scalar.activation(
-                out=relu[:].rearrange("p t m j -> p m j t"),
-                in_=pieces[i].rearrange("p j (m t) -> p m j t", t=T),
-                func=ACT.Relu,
+        def load_weight(engine, h):
+            engine.dma_start(out=weight[ROWS * h : ROWS * (h + 1), :], in_=qa_v)
+
+        def warm_up():
+            warm_in = sb.tile([P, 1], F32, name="warm_in")
+            warm_out = sb.tile([P, 1], F32, name="warm_out")
+            nc.vector.memset(warm_in[:], 0.0)
+            nc.scalar.activation(out=warm_out[:], in_=warm_in[:], func=ACT.Sigmoid)
+
+        def load_q(c):
+            q_raw[c] = sb.tile([P, PACK, CHUNK], F32, name="q_raw%d" % c)
+            nc.sync.dma_start(out=q_raw[c][:], in_=q_v[:, :, CHUNK * c : CHUNK * (c + 1)])
+
+        def load_state():
+            nc.sync.dma_start(out=s_raw[:], in_=s_v)
+
+        def load_gate(g, k):
+            gate[g, k] = sb.tile([P, PAIR, T * E], F32, name="gate%d_%d" % (g, k))
+            nc.sync.dma_start(out=gate[g, k][:], in_=og_v[g, :, PAIR * k : PAIR * (k + 1), :])
+
+        def round_state_vector():
+            nc.vector.tensor_copy(out=s_bf[:], in_=s_raw[:].rearrange("p j e -> p e j"))
+
+        def round_state_scalar():
+            nc.scalar.copy(
+                out=s_bf[:].rearrange("p (c i) j -> p c j i", i=4),
+                in_=s_raw[:].rearrange("p j (c i) -> p c j i", i=4),
             )
+
+        def quantize_state():
+            nc.vector.quantize_mx(out=s_codes[:].bitcast(FP8X4), scales=s_scales[:], in_=s_bf[:].rearrange("p e j -> p (e j)"))
+
+        def rectify(n0, width, on_vector=False):
+            c, o = divmod(n0, CHUNK)
+            relu[n0] = sb.tile([P, T, width // T, PACK], F32, name="relu%d" % n0)
+            dst = relu[n0][:].rearrange("p t m j -> p m j t")
+            src = q_raw[c][:, :, o : o + width].rearrange("p j (m t) -> p m j t", t=T)
+            if on_vector:
+                nc.vector.tensor_scalar_max(out=dst, in0=src, scalar1=0.0)
+            else:
+                nc.scalar.activation(out=dst, in_=src, func=ACT.Relu)
+
+        def weigh(n0, width, t0=0, t1=T):
+            g, m0 = divmod(n0 // T, P)
             nc.vector.scalar_tensor_tensor(
-                out=fq[g][:, :, m0 : m0 + MP, :].rearrange("p t m j -> p t (m j)"),
-                in0=relu[:].rearrange("p t m j -> p t (m j)"),
+                out=fq[g][:, t0:t1, m0 : m0 + width // T, :].rearrange("p t m j -> p t (m j)"),
+                in0=relu[n0][:, t0:t1].rearrange("p t m j -> p t (m j)"),
                 scalar=0.125,
-                in1=weight[:].unsqueeze(1).to_broadcast([P, T * MP, PACK]),
+                in1=weight[:].unsqueeze(1).to_broadcast([P, (t1 - t0) * width // T, PACK]),
                 op0=ALU.add,
                 op1=ALU.mult,
             )
 
-        def multiply(g):
+        def quantize(g, t0=0, t1=T):
             nc.vector.quantize_mx(
-                out=q_codes[g][:].rearrange("p t m -> p (t m)").bitcast(FP8X4),
-                scales=q_scales[g][:].rearrange("p t m -> p (t m)"),
-                in_=fq[g][:].rearrange("p t m j -> p (t m j)"),
+                out=q_codes[g][:, t0:t1].rearrange("p t m -> p (t m)").bitcast(FP8X4),
+                scales=q_scales[g][:, t0:t1].rearrange("p t m -> p (t m)"),
+                in_=fq[g][:, t0:t1].rearrange("p t m j -> p (t m j)"),
             )
+
+        def multiply(g):
             for k in range(H // PAIR):
                 for t in range(T):
                     for h in range(PAIR * k, PAIR * (k + 1)):
@@ -128,13 +127,10 @@ def tile_rows_read_relu1_gate_kernel(tc, q, qa, S, og, out):
                             stop=True,
                         )
 
-        sig = {}
+        def sigmoid(g, h, c0=0, c1=T * E):
+            nc.scalar.activation(out=sig[g, h][:, c0:c1], in_=gate[g, h // PAIR][:, h % PAIR, c0:c1], func=ACT.Sigmoid)
 
-        def sigmoid(g, h):
-            sig[g, h] = sb.tile([P, T * E], F32, name="sig%d_%d" % (g, h))
-            nc.scalar.activation(out=sig[g, h][:], in_=gate[g, h // PAIR][:, h % PAIR, :], func=ACT.Sigmoid)
-
-        def gate_vector(g, h, c0=0, c1=T * E):
+        def apply_gate(g, h, c0=0, c1=T * E):
             nc.vector.tensor_tensor(
                 out=res[g, h // PAIR][:, h % PAIR, c0:c1],
                 in0=banks[g, h][:].rearrange("p t e -> p (t e)")[:, c0:c1],
@@ -142,54 +138,71 @@ def tile_rows_read_relu1_gate_kernel(tc, q, qa, S, og, out):
                 op=ALU.mult,
             )
 
-        sums = {}
+        def store_pair(g, k, engine=nc.sync):
+            engine.dma_start(out=out_v[g, :, PAIR * k : PAIR * (k + 1), :], in_=res[g, k][:])
 
-        def copy_out(g, h):
-            sums[g, h] = sb.tile([P, T * E], F32, name="sums%d_%d" % (g, h))
-            nc.scalar.copy(out=sums[g, h][:], in_=banks[g, h][:].rearrange("p t e -> p (t e)"))
+        def store_head(g, h, engine=nc.sync):
+            engine.dma_start(out=out_v[g, :, h, :], in_=res[g, h // PAIR][:, h % PAIR, :])
 
-        def gate_gpsimd(g, h):
-            nc.gpsimd.tensor_tensor(out=res[g, h // PAIR][:, h % PAIR, :], in0=sums[g, h][:], in1=sig[g, h][:], op=ALU.mult)
+        def gate_on_gpsimd(g, h, c0=0, c1=T * E):
+            sums = sb.tile([P, c1 - c0], F32, name="sums%d_%d" % (g, h))
+            nc.scalar.copy(out=sums[:], in_=banks[g, h][:].rearrange("p t e -> p (t e)")[:, c0:c1])
+            nc.gpsimd.tensor_tensor(out=res[g, h // PAIR][:, h % PAIR, c0:c1], in0=sums[:], in1=sig[g, h][:, c0:c1], op=ALU.mult)
 
-        def store_pair(g, k):
-            nc.sync.dma_start(out=out_v[g, :, PAIR * k : PAIR * (k + 1), :], in_=res[g, k][:])
-
-        def store_head(g, h, c0=0, c1=T * E):
-            nc.sync.dma_start(out=out_v[g, :, h, c0:c1], in_=res[g, h // PAIR][:, h % PAIR, c0:c1])
-
-        feature_map(0)
-        feature_map(1)
-        round_state()
-        feature_map(2)
-        feature_map(3)
+        load_weight(nc.scalar, 0)
+        load_weight(nc.scalar, 1)
+        warm_up()
+        load_q(0)
+        load_weight(nc.sync, 2)
+        load_weight(nc.sync, 3)
+        load_q(1)
+        load_state()
+        load_q(2)
+        load_q(3)
+        for g in range(GROUPS):
+            for k in range(H // PAIR):
+                load_gate(g, k)
+        rectify(0, 64)
+        rectify(64, 128, on_vector=True)
+        rectify(192, 64)
+        weigh(0, 64)
+        weigh(64, 128)
+        weigh(192, 64)
+        rectify(256, 128)
+        rectify(384, 128)
+        round_state_scalar()
+        weigh(256, 128)
+        weigh(384, 128, 0, 2)
+        weigh(384, 128, 2, 4)
+        rectify(512, 128)
+        rectify(640, 128)
+        quantize(0, 0, 2)
+        quantize(0, 2, 4)
         quantize_state()
         multiply(0)
-        feature_map(4)
-        feature_map(5)
-        feature_map(6)
-        feature_map(7)
-        sigmoid(0, 0)
-        gate_vector(0, 0)
-        store_head(0, 0)
-        sigmoid(0, 1)
-        gate_vector(0, 1)
-        store_head(0, 1)
+        weigh(512, 128)
+        weigh(640, 128)
+        rectify(768, 64)
+        rectify(832, 64, on_vector=True)
+        rectify(896, 128)
+        weigh(768, 64)
+        weigh(832, 64)
+        weigh(896, 128, 0, 2)
+        weigh(896, 128, 2, 4)
+        quantize(1, 0, 2)
+        quantize(1, 2, 4)
         multiply(1)
-        sigmoid(0, 2)
-        gate_vector(0, 2)
-        store_head(0, 2)
+        for h in range(H - 1):
+            sigmoid(0, h)
+            apply_gate(0, h)
+            store_head(0, h)
         sigmoid(0, 3)
-        gate_vector(0, 3)
-        store_head(0, 3)
+        gate_on_gpsimd(0, 3)
         sigmoid(1, 0)
-        gate_vector(1, 0)
+        apply_gate(1, 0)
+        store_head(0, 3)
         store_head(1, 0)
-        sigmoid(1, 1)
-        gate_vector(1, 1)
-        store_head(1, 1)
-        sigmoid(1, 2)
-        gate_vector(1, 2)
-        store_head(1, 2)
-        sigmoid(1, 3)
-        gate_vector(1, 3)
-        store_head(1, 3)
+        for h in range(1, H):
+            sigmoid(1, h)
+            apply_gate(1, h)
+            store_head(1, h)

@@ -68,9 +68,11 @@ def tile_rows_read_relu1_gate_kernel(tc, q, qa, S, og, out):
         def load_state():
             nc.sync.dma_start(out=s_raw[:], in_=s_v)
 
-        def load_gate(g, k):
-            gate[g, k] = sb.tile([P, PAIR, T * E], F32, name="gate%d_%d" % (g, k))
-            nc.sync.dma_start(out=gate[g, k][:], in_=og_v[g, :, PAIR * k : PAIR * (k + 1), :])
+        def load_gate(g, h0, h1):
+            tile = sb.tile([P, h1 - h0, T * E], F32, name="gate%d_%d" % (g, h0))
+            nc.sync.dma_start(out=tile[:], in_=og_v[g, :, h0:h1, :])
+            for h in range(h0, h1):
+                gate[g, h] = tile[:, h - h0, :]
 
         def round_state_vector():
             nc.vector.tensor_copy(out=s_bf[:], in_=s_raw[:].rearrange("p j e -> p e j"))
@@ -128,7 +130,7 @@ def tile_rows_read_relu1_gate_kernel(tc, q, qa, S, og, out):
                         )
 
         def sigmoid(g, h, c0=0, c1=T * E):
-            nc.scalar.activation(out=sig[g, h][:, c0:c1], in_=gate[g, h // PAIR][:, h % PAIR, c0:c1], func=ACT.Sigmoid)
+            nc.scalar.activation(out=sig[g, h][:, c0:c1], in_=gate[g, h][:, c0:c1], func=ACT.Sigmoid)
 
         def apply_gate(g, h, c0=0, c1=T * E):
             nc.vector.tensor_tensor(
@@ -144,11 +146,6 @@ def tile_rows_read_relu1_gate_kernel(tc, q, qa, S, og, out):
         def store_head(g, h, engine=nc.sync):
             engine.dma_start(out=out_v[g, :, h, :], in_=res[g, h // PAIR][:, h % PAIR, :])
 
-        def gate_on_gpsimd(g, h, c0=0, c1=T * E):
-            sums = sb.tile([P, c1 - c0], F32, name="sums%d_%d" % (g, h))
-            nc.scalar.copy(out=sums[:], in_=banks[g, h][:].rearrange("p t e -> p (t e)")[:, c0:c1])
-            nc.gpsimd.tensor_tensor(out=res[g, h // PAIR][:, h % PAIR, c0:c1], in0=sums[:], in1=sig[g, h][:, c0:c1], op=ALU.mult)
-
         load_weight(nc.scalar, 0)
         load_weight(nc.scalar, 1)
         warm_up()
@@ -156,53 +153,49 @@ def tile_rows_read_relu1_gate_kernel(tc, q, qa, S, og, out):
         load_weight(nc.sync, 2)
         load_weight(nc.sync, 3)
         load_q(1)
-        load_state()
         load_q(2)
+        load_state()
         load_q(3)
-        for g in range(GROUPS):
-            for k in range(H // PAIR):
-                load_gate(g, k)
+        load_gate(0, 0, 1)
+        load_gate(0, 1, 2)
+        load_gate(0, 2, 4)
+        load_gate(1, 0, 2)
+        load_gate(1, 2, 3)
+        load_gate(1, 3, 4)
         rectify(0, 64)
         rectify(64, 128, on_vector=True)
         rectify(192, 64)
         weigh(0, 64)
         weigh(64, 128)
         weigh(192, 64)
-        rectify(256, 128)
+        rectify(256, 64)
+        rectify(320, 64)
         rectify(384, 128)
-        round_state_scalar()
-        weigh(256, 128)
+        weigh(256, 64)
+        weigh(320, 64)
         weigh(384, 128, 0, 2)
         weigh(384, 128, 2, 4)
         rectify(512, 128)
         rectify(640, 128)
+        round_state_scalar()
         quantize(0, 0, 2)
         quantize(0, 2, 4)
-        quantize_state()
-        multiply(0)
         weigh(512, 128)
         weigh(640, 128)
+        quantize_state()
+        multiply(0)
         rectify(768, 64)
-        rectify(832, 64, on_vector=True)
-        rectify(896, 128)
+        rectify(832, 128, on_vector=True)
+        rectify(960, 64)
         weigh(768, 64)
-        weigh(832, 64)
-        weigh(896, 128, 0, 2)
-        weigh(896, 128, 2, 4)
+        weigh(960, 64)
+        weigh(832, 128, 0, 2)
+        weigh(832, 128, 2, 4)
         quantize(1, 0, 2)
         quantize(1, 2, 4)
         multiply(1)
-        for h in range(H - 1):
-            sigmoid(0, h)
-            apply_gate(0, h)
-            store_head(0, h)
-        sigmoid(0, 3)
-        gate_on_gpsimd(0, 3)
-        sigmoid(1, 0)
-        apply_gate(1, 0)
-        store_head(0, 3)
-        store_head(1, 0)
-        for h in range(1, H):
-            sigmoid(1, h)
-            apply_gate(1, h)
-            store_head(1, h)
+        for g in range(GROUPS):
+            for h in range(H):
+                sigmoid(g, h)
+                apply_gate(g, h)
+                store_head(g, h)

@@ -19,8 +19,10 @@ ROWS = D // PACK
 T = 4
 GROUP = P * T
 GROUPS = N // GROUP
+HALF = GROUP // 2
 PAIR = 2
-CHUNK = 256
+OFFSET = 0.125
+FAR = 3.0e38
 
 
 def tile_rows_read_relu1_gate_kernel(tc, q, qa, S, og, out):
@@ -37,20 +39,25 @@ def tile_rows_read_relu1_gate_kernel(tc, q, qa, S, og, out):
         ctx.enter_context(tc.manual_schedule())
 
         weight = sb.tile([P, PACK], F32, name="weight")
+        base = sb.tile([P, PACK], F32, name="base")
+        side = sb.tile([P, PACK], F32, name="side")
+        lower = sb.tile([P, PACK], F32, name="lower")
+        upper = sb.tile([P, PACK], F32, name="upper")
         s_raw = sb.tile([P, PACK, E], F32, name="s_raw")
         s_bf = sb.tile([P, E, PACK], BF16, name="s_bf", align_bytes=64)
         s_codes = sb.tile([P, E], U32, name="s_codes", align_bytes=64)
         s_scales = sb.tile([P, E], U8, name="s_scales", align_bytes=64)
-        q_raw, gate, fq, q_codes, q_scales, banks, res, sig, relu = {}, {}, {}, {}, {}, {}, {}, {}, {}
+        q_raw, gate, line, fq, q_codes, q_scales, banks, res, sig = {}, {}, {}, {}, {}, {}, {}, {}, {}
         for g in range(GROUPS):
+            for half in range(2):
+                line[g, half] = sb.tile([P, PACK, HALF], BF16, name="line%d_%d" % (g, half), align_bytes=64)
             fq[g] = sb.tile([P, T, P, PACK], BF16, name="fq%d" % g, align_bytes=64)
             q_codes[g] = sb.tile([P, T, P], U32, name="q_codes%d" % g, align_bytes=64)
             q_scales[g] = sb.tile([P, T, P], U8, name="q_scales%d" % g, align_bytes=64)
             for h in range(H):
                 banks[g, h] = ps.tile([P, T, E], F32, name="y%d_%d" % (g, h))
                 sig[g, h] = sb.tile([P, T * E], F32, name="sig%d_%d" % (g, h))
-            for k in range(H // PAIR):
-                res[g, k] = sb.tile([P, PAIR, T * E], F32, name="res%d_%d" % (g, k))
+                res[g, h] = sb.tile([P, T * E], F32, name="res%d_%d" % (g, h))
 
         def load_weight(engine, h):
             engine.dma_start(out=weight[ROWS * h : ROWS * (h + 1), :], in_=qa_v)
@@ -61,23 +68,28 @@ def tile_rows_read_relu1_gate_kernel(tc, q, qa, S, og, out):
             nc.vector.memset(warm_in[:], 0.0)
             nc.scalar.activation(out=warm_out[:], in_=warm_in[:], func=ACT.Sigmoid)
 
-        def load_q(c):
-            q_raw[c] = sb.tile([P, PACK, CHUNK], F32, name="q_raw%d" % c)
-            nc.sync.dma_start(out=q_raw[c][:], in_=q_v[:, :, CHUNK * c : CHUNK * (c + 1)])
+        def bounds():
+            nc.vector.tensor_scalar_mul(out=base[:], in0=weight[:], scalar1=OFFSET)
+            nc.vector.tensor_scalar(out=side[:], in0=weight[:], scalar1=0.0, scalar2=0.5, op0=ALU.is_ge, op1=ALU.subtract)
+            nc.vector.scalar_tensor_tensor(out=lower[:], in0=side[:], scalar=FAR, in1=base[:], op0=ALU.mult, op1=ALU.min)
+            nc.vector.scalar_tensor_tensor(out=upper[:], in0=side[:], scalar=FAR, in1=base[:], op0=ALU.mult, op1=ALU.max)
+
+        def load_q(g, j0, j1):
+            tile = sb.tile([P, j1 - j0, GROUP], F32, name="q_raw%d_%d" % (g, j0))
+            nc.sync.dma_start(out=tile[:], in_=q_v[:, j0:j1, GROUP * g : GROUP * (g + 1)])
+            for j in range(j0, j1):
+                q_raw[g, j] = tile[:, j - j0, :]
 
         def load_state():
             nc.sync.dma_start(out=s_raw[:], in_=s_v)
 
-        def load_gate(g, h0, h1):
+        def load_gate(g, h0, h1, engine=nc.sync):
             tile = sb.tile([P, h1 - h0, T * E], F32, name="gate%d_%d" % (g, h0))
-            nc.sync.dma_start(out=tile[:], in_=og_v[g, :, h0:h1, :])
+            engine.dma_start(out=tile[:], in_=og_v[g, :, h0:h1, :])
             for h in range(h0, h1):
                 gate[g, h] = tile[:, h - h0, :]
 
-        def round_state_vector():
-            nc.vector.tensor_copy(out=s_bf[:], in_=s_raw[:].rearrange("p j e -> p e j"))
-
-        def round_state_scalar():
+        def round_state():
             nc.scalar.copy(
                 out=s_bf[:].rearrange("p (c i) j -> p c j i", i=4),
                 in_=s_raw[:].rearrange("p j (c i) -> p c j i", i=4),
@@ -86,26 +98,43 @@ def tile_rows_read_relu1_gate_kernel(tc, q, qa, S, og, out):
         def quantize_state():
             nc.vector.quantize_mx(out=s_codes[:].bitcast(FP8X4), scales=s_scales[:], in_=s_bf[:].rearrange("p e j -> p (e j)"))
 
-        def rectify(n0, width, on_vector=False):
-            c, o = divmod(n0, CHUNK)
-            relu[n0] = sb.tile([P, T, width // T, PACK], F32, name="relu%d" % n0)
-            dst = relu[n0][:].rearrange("p t m j -> p m j t")
-            src = q_raw[c][:, :, o : o + width].rearrange("p j (m t) -> p m j t", t=T)
-            if on_vector:
-                nc.vector.tensor_scalar_max(out=dst, in0=src, scalar1=0.0)
-            else:
-                nc.scalar.activation(out=dst, in_=src, func=ACT.Relu)
-
-        def weigh(n0, width, t0=0, t1=T):
-            g, m0 = divmod(n0 // T, P)
-            nc.vector.scalar_tensor_tensor(
-                out=fq[g][:, t0:t1, m0 : m0 + width // T, :].rearrange("p t m j -> p t (m j)"),
-                in0=relu[n0][:, t0:t1].rearrange("p t m j -> p t (m j)"),
-                scalar=0.125,
-                in1=weight[:].unsqueeze(1).to_broadcast([P, (t1 - t0) * width // T, PACK]),
-                op0=ALU.add,
-                op1=ALU.mult,
+        def weigh_scalar(g, half, j):
+            nc.scalar.activation(
+                out=line[g, half][:, j, :],
+                in_=q_raw[g, j][:, HALF * half : HALF * (half + 1)],
+                func=ACT.Identity,
+                scale=weight[:, j : j + 1],
+                bias=base[:, j : j + 1],
             )
+
+        def weigh_vector(g, half, j):
+            nc.vector.tensor_scalar(
+                out=line[g, half][:, j, :],
+                in0=q_raw[g, j][:, HALF * half : HALF * (half + 1)],
+                scalar1=weight[:, j : j + 1],
+                scalar2=base[:, j : j + 1],
+                op0=ALU.mult,
+                op1=ALU.add,
+            )
+
+        def clamp(g, half, j):
+            nc.vector.tensor_scalar(
+                out=line[g, half][:, j, :],
+                in0=line[g, half][:, j, :],
+                scalar1=lower[:, j : j + 1],
+                scalar2=upper[:, j : j + 1],
+                op0=ALU.max,
+                op1=ALU.min,
+            )
+
+        def interleave(g, half, t0=0, t1=T, on_scalar=False):
+            m0 = half * HALF // T
+            dst = fq[g][:, t0:t1, m0 : m0 + HALF // T, :].rearrange("p t m j -> p m j t")
+            src = line[g, half][:].rearrange("p j (m t) -> p m j t", t=T)[:, :, :, t0:t1]
+            if on_scalar:
+                nc.scalar.copy(out=dst, in_=src)
+            else:
+                nc.vector.tensor_copy(out=dst, in_=src)
 
         def quantize(g, t0=0, t1=T):
             nc.vector.quantize_mx(
@@ -129,73 +158,84 @@ def tile_rows_read_relu1_gate_kernel(tc, q, qa, S, og, out):
                             stop=True,
                         )
 
-        def sigmoid(g, h, c0=0, c1=T * E):
-            nc.scalar.activation(out=sig[g, h][:, c0:c1], in_=gate[g, h][:, c0:c1], func=ACT.Sigmoid)
+        def sigmoid(g, h):
+            nc.scalar.activation(out=sig[g, h][:], in_=gate[g, h], func=ACT.Sigmoid)
 
-        def apply_gate(g, h, c0=0, c1=T * E):
+        def apply_gate(g, h):
             nc.vector.tensor_tensor(
-                out=res[g, h // PAIR][:, h % PAIR, c0:c1],
-                in0=banks[g, h][:].rearrange("p t e -> p (t e)")[:, c0:c1],
-                in1=sig[g, h][:, c0:c1],
+                out=res[g, h][:],
+                in0=banks[g, h][:].rearrange("p t e -> p (t e)"),
+                in1=sig[g, h][:],
                 op=ALU.mult,
             )
 
-        def store_pair(g, k, engine=nc.sync):
-            engine.dma_start(out=out_v[g, :, PAIR * k : PAIR * (k + 1), :], in_=res[g, k][:])
-
-        def store_head(g, h, engine=nc.sync):
-            engine.dma_start(out=out_v[g, :, h, :], in_=res[g, h // PAIR][:, h % PAIR, :])
+        def store(g, h, engine=nc.sync):
+            engine.dma_start(out=out_v[g, :, h, :], in_=res[g, h][:])
 
         load_weight(nc.scalar, 0)
         load_weight(nc.scalar, 1)
         warm_up()
-        load_q(0)
+        load_q(0, 0, 2)
         load_weight(nc.sync, 2)
         load_weight(nc.sync, 3)
-        load_q(1)
-        load_q(2)
+        load_q(0, 2, 4)
         load_state()
-        load_q(3)
+        load_q(1, 0, 2)
+        load_q(1, 2, 4)
         load_gate(0, 0, 1)
         load_gate(0, 1, 2)
         load_gate(0, 2, 4)
         load_gate(1, 0, 2)
         load_gate(1, 2, 3)
         load_gate(1, 3, 4)
-        rectify(0, 64)
-        rectify(64, 128, on_vector=True)
-        rectify(192, 64)
-        weigh(0, 64)
-        weigh(64, 128)
-        weigh(192, 64)
-        rectify(256, 64)
-        rectify(320, 64)
-        rectify(384, 128)
-        weigh(256, 64)
-        weigh(320, 64)
-        weigh(384, 128, 0, 2)
-        weigh(384, 128, 2, 4)
-        rectify(512, 128)
-        rectify(640, 128)
-        round_state_scalar()
-        quantize(0, 0, 2)
-        quantize(0, 2, 4)
-        weigh(512, 128)
-        weigh(640, 128)
+        bounds()
+        for half in range(2):
+            weigh_scalar(0, half, 0)
+            weigh_vector(0, half, 1)
+        for half in range(2):
+            clamp(0, half, 1)
+        weigh_scalar(0, 0, 2)
+        weigh_vector(0, 0, 3)
+        for half in range(2):
+            clamp(0, half, 0)
+        weigh_scalar(0, 1, 2)
+        weigh_scalar(0, 1, 3)
+        round_state()
+        clamp(0, 0, 2)
+        clamp(0, 0, 3)
+        clamp(0, 1, 2)
+        interleave(0, 0)
+        clamp(0, 1, 3)
         quantize_state()
+        interleave(0, 1)
+        for half in range(2):
+            for j in range(2):
+                weigh_scalar(1, half, j)
+        clamp(1, 0, 0)
+        clamp(1, 0, 1)
+        quantize(0)
         multiply(0)
-        rectify(768, 64)
-        rectify(832, 128, on_vector=True)
-        rectify(960, 64)
-        weigh(768, 64)
-        weigh(960, 64)
-        weigh(832, 128, 0, 2)
-        weigh(832, 128, 2, 4)
-        quantize(1, 0, 2)
-        quantize(1, 2, 4)
+        weigh_scalar(1, 0, 2)
+        weigh_vector(1, 0, 3)
+        weigh_scalar(1, 1, 2)
+        weigh_scalar(1, 1, 3)
+        clamp(1, 1, 0)
+        clamp(1, 1, 1)
+        clamp(1, 0, 2)
+        clamp(1, 0, 3)
+        clamp(1, 1, 2)
+        clamp(1, 1, 3)
+        sigmoid(0, 0)
+        interleave(1, 0)
+        interleave(1, 1, 2, 4, on_scalar=True)
+        interleave(1, 1, 0, 2)
+        apply_gate(0, 0)
+        store(0, 0)
+        quantize(1)
         multiply(1)
         for g in range(GROUPS):
             for h in range(H):
-                sigmoid(g, h)
-                apply_gate(g, h)
-                store_head(g, h)
+                if (g, h) != (0, 0):
+                    sigmoid(g, h)
+                    apply_gate(g, h)
+                    store(g, h)

@@ -19,7 +19,6 @@ ROWS = D // PACK
 T = 4
 GROUP = P * T
 GROUPS = N // GROUP
-HALF = GROUP // 2
 PAIR = 2
 OFFSET = 0.125
 FAR = 3.0e38
@@ -49,8 +48,7 @@ def tile_rows_read_relu1_gate_kernel(tc, q, qa, S, og, out):
         s_scales = sb.tile([P, E], U8, name="s_scales", align_bytes=64)
         q_raw, gate, line, fq, q_codes, q_scales, banks, res, sig = {}, {}, {}, {}, {}, {}, {}, {}, {}
         for g in range(GROUPS):
-            for half in range(2):
-                line[g, half] = sb.tile([P, PACK, HALF], BF16, name="line%d_%d" % (g, half), align_bytes=64)
+            line[g] = sb.tile([P, PACK, GROUP], BF16, name="line%d" % g, align_bytes=64)
             fq[g] = sb.tile([P, T, P, PACK], BF16, name="fq%d" % g, align_bytes=64)
             q_codes[g] = sb.tile([P, T, P], U32, name="q_codes%d" % g, align_bytes=64)
             q_scales[g] = sb.tile([P, T, P], U8, name="q_scales%d" % g, align_bytes=64)
@@ -90,7 +88,7 @@ def tile_rows_read_relu1_gate_kernel(tc, q, qa, S, og, out):
                 gate[g, h] = tile[:, h - h0, :]
 
         def round_state():
-            nc.scalar.copy(
+            nc.vector.tensor_copy(
                 out=s_bf[:].rearrange("p (c i) j -> p c j i", i=4),
                 in_=s_raw[:].rearrange("p j (c i) -> p c j i", i=4),
             )
@@ -98,43 +96,46 @@ def tile_rows_read_relu1_gate_kernel(tc, q, qa, S, og, out):
         def quantize_state():
             nc.vector.quantize_mx(out=s_codes[:].bitcast(FP8X4), scales=s_scales[:], in_=s_bf[:].rearrange("p e j -> p (e j)"))
 
-        def weigh_scalar(g, half, j):
+        def weigh_scalar(g, j):
             nc.scalar.activation(
-                out=line[g, half][:, j, :],
-                in_=q_raw[g, j][:, HALF * half : HALF * (half + 1)],
+                out=line[g][:, j, :],
+                in_=q_raw[g, j],
                 func=ACT.Identity,
                 scale=weight[:, j : j + 1],
                 bias=base[:, j : j + 1],
             )
 
-        def weigh_vector(g, half, j):
+        def weigh_vector(g, j):
             nc.vector.tensor_scalar(
-                out=line[g, half][:, j, :],
-                in0=q_raw[g, j][:, HALF * half : HALF * (half + 1)],
+                out=line[g][:, j, :],
+                in0=q_raw[g, j],
                 scalar1=weight[:, j : j + 1],
                 scalar2=base[:, j : j + 1],
                 op0=ALU.mult,
                 op1=ALU.add,
             )
 
-        def clamp(g, half, j):
+        def clamp(g, j):
             nc.vector.tensor_scalar(
-                out=line[g, half][:, j, :],
-                in0=line[g, half][:, j, :],
+                out=line[g][:, j, :],
+                in0=line[g][:, j, :],
                 scalar1=lower[:, j : j + 1],
                 scalar2=upper[:, j : j + 1],
                 op0=ALU.max,
                 op1=ALU.min,
             )
 
-        def interleave(g, half, t0=0, t1=T, on_scalar=False):
-            m0 = half * HALF // T
-            dst = fq[g][:, t0:t1, m0 : m0 + HALF // T, :].rearrange("p t m j -> p m j t")
-            src = line[g, half][:].rearrange("p j (m t) -> p m j t", t=T)[:, :, :, t0:t1]
-            if on_scalar:
-                nc.scalar.copy(out=dst, in_=src)
-            else:
-                nc.vector.tensor_copy(out=dst, in_=src)
+        def interleave_vector(g, t0, t1):
+            nc.vector.tensor_copy(
+                out=fq[g][:, t0:t1].rearrange("p t (c i) j -> p c j i t", i=2),
+                in_=line[g][:].rearrange("p j (c i t) -> p c j i t", i=2, t=T)[:, :, :, :, t0:t1],
+            )
+
+        def interleave_scalar(g, t):
+            nc.scalar.copy(
+                out=fq[g][:, t].rearrange("p (c i) j -> p c j i", i=2),
+                in_=line[g][:].rearrange("p j (c i t) -> p c j i t", i=2, t=T)[:, :, :, :, t],
+            )
 
         def quantize(g, t0=0, t1=T):
             nc.vector.quantize_mx(
@@ -189,46 +190,31 @@ def tile_rows_read_relu1_gate_kernel(tc, q, qa, S, og, out):
         load_gate(1, 2, 3)
         load_gate(1, 3, 4)
         bounds()
-        for half in range(2):
-            weigh_scalar(0, half, 0)
-            weigh_vector(0, half, 1)
-        for half in range(2):
-            clamp(0, half, 1)
-        weigh_scalar(0, 0, 2)
-        weigh_vector(0, 0, 3)
-        for half in range(2):
-            clamp(0, half, 0)
-        weigh_scalar(0, 1, 2)
-        weigh_scalar(0, 1, 3)
+        weigh_scalar(0, 0)
+        weigh_vector(0, 1)
+        clamp(0, 1)
+        weigh_scalar(0, 2)
+        weigh_vector(0, 3)
+        clamp(0, 0)
+        clamp(0, 3)
+        clamp(0, 2)
         round_state()
-        clamp(0, 0, 2)
-        clamp(0, 0, 3)
-        clamp(0, 1, 2)
-        interleave(0, 0)
-        clamp(0, 1, 3)
+        interleave_scalar(0, 3)
+        interleave_vector(0, 0, 3)
         quantize_state()
-        interleave(0, 1)
-        for half in range(2):
-            for j in range(2):
-                weigh_scalar(1, half, j)
-        clamp(1, 0, 0)
-        clamp(1, 0, 1)
         quantize(0)
         multiply(0)
-        weigh_scalar(1, 0, 2)
-        weigh_vector(1, 0, 3)
-        weigh_scalar(1, 1, 2)
-        weigh_scalar(1, 1, 3)
-        clamp(1, 1, 0)
-        clamp(1, 1, 1)
-        clamp(1, 0, 2)
-        clamp(1, 0, 3)
-        clamp(1, 1, 2)
-        clamp(1, 1, 3)
+        weigh_scalar(1, 0)
+        weigh_scalar(1, 1)
+        weigh_scalar(1, 2)
+        weigh_vector(1, 3)
+        clamp(1, 0)
+        clamp(1, 1)
+        clamp(1, 3)
+        clamp(1, 2)
         sigmoid(0, 0)
-        interleave(1, 0)
-        interleave(1, 1, 2, 4, on_scalar=True)
-        interleave(1, 1, 0, 2)
+        interleave_scalar(1, 3)
+        interleave_vector(1, 0, 3)
         apply_gate(0, 0)
         store(0, 0)
         quantize(1)

@@ -19,6 +19,7 @@ ROWS = D // PACK
 T = 4
 GROUP = P * T
 GROUPS = N // GROUP
+HALF = GROUP // 2
 PAIR = 2
 OFFSET = 0.125
 FAR = 3.0e38
@@ -40,15 +41,15 @@ def tile_rows_read_relu1_gate_kernel(tc, q, qa, S, og, out):
         weight = sb.tile([P, PACK], F32, name="weight")
         base = sb.tile([P, PACK], F32, name="base")
         side = sb.tile([P, PACK], F32, name="side")
-        lower = sb.tile([P, PACK], F32, name="lower")
-        upper = sb.tile([P, PACK], F32, name="upper")
+        lower = sb.tile([P, PACK], BF16, name="lower")
+        upper = sb.tile([P, PACK], BF16, name="upper")
         s_raw = sb.tile([P, PACK, E], F32, name="s_raw")
         s_bf = sb.tile([P, E, PACK], BF16, name="s_bf", align_bytes=64)
         s_codes = sb.tile([P, E], U32, name="s_codes", align_bytes=64)
         s_scales = sb.tile([P, E], U8, name="s_scales", align_bytes=64)
         q_raw, gate, line, fq, q_codes, q_scales, banks, res, sig = {}, {}, {}, {}, {}, {}, {}, {}, {}
         for g in range(GROUPS):
-            line[g] = sb.tile([P, PACK, GROUP], BF16, name="line%d" % g, align_bytes=64)
+            line[g] = sb.tile([P, 2, PACK, HALF], BF16, name="line%d" % g, align_bytes=64)
             fq[g] = sb.tile([P, T, P, PACK], BF16, name="fq%d" % g, align_bytes=64)
             q_codes[g] = sb.tile([P, T, P], U32, name="q_codes%d" % g, align_bytes=64)
             q_scales[g] = sb.tile([P, T, P], U8, name="q_scales%d" % g, align_bytes=64)
@@ -78,6 +79,18 @@ def tile_rows_read_relu1_gate_kernel(tc, q, qa, S, og, out):
             for j in range(j0, j1):
                 q_raw[g, j] = tile[:, j - j0, :]
 
+        def load_cols(g, half):
+            tile = sb.tile([P, PACK, HALF], F32, name="q_cols%d_%d" % (g, half))
+            n0 = GROUP * g + HALF * half
+            nc.sync.dma_start(out=tile[:], in_=q_v[:, :, n0 : n0 + HALF])
+            for j in range(PACK):
+                q_raw[g, j, half] = tile[:, j : j + 1, :]
+
+        def source(g, j, h0, h1):
+            if (g, j, h0) in q_raw:
+                return q_raw[g, j, h0]
+            return halves(q_raw[g, j], h0, h1)
+
         def load_state():
             nc.sync.dma_start(out=s_raw[:], in_=s_v)
 
@@ -87,8 +100,8 @@ def tile_rows_read_relu1_gate_kernel(tc, q, qa, S, og, out):
             for h in range(h0, h1):
                 gate[g, h] = tile[:, h - h0, :]
 
-        def round_state():
-            nc.vector.tensor_copy(
+        def round_state(copy):
+            copy(
                 out=s_bf[:].rearrange("p (c i) j -> p c j i", i=4),
                 in_=s_raw[:].rearrange("p j (c i) -> p c j i", i=4),
             )
@@ -96,46 +109,54 @@ def tile_rows_read_relu1_gate_kernel(tc, q, qa, S, og, out):
         def quantize_state():
             nc.vector.quantize_mx(out=s_codes[:].bitcast(FP8X4), scales=s_scales[:], in_=s_bf[:].rearrange("p e j -> p (e j)"))
 
-        def weigh_scalar(g, j):
+        def halves(row, h0, h1):
+            return row.rearrange("p (a n) -> p a n", a=2)[:, h0:h1, :]
+
+        def weigh_scalar(g, j, h0=0, h1=2):
             nc.scalar.activation(
-                out=line[g][:, j, :],
-                in_=q_raw[g, j],
+                out=line[g][:, h0:h1, j, :],
+                in_=source(g, j, h0, h1),
                 func=ACT.Identity,
                 scale=weight[:, j : j + 1],
                 bias=base[:, j : j + 1],
             )
 
-        def weigh_vector(g, j):
+        def weigh_vector(g, j, h0=0, h1=2):
             nc.vector.tensor_scalar(
-                out=line[g][:, j, :],
-                in0=q_raw[g, j],
+                out=line[g][:, h0:h1, j, :],
+                in0=source(g, j, h0, h1),
                 scalar1=weight[:, j : j + 1],
                 scalar2=base[:, j : j + 1],
                 op0=ALU.mult,
                 op1=ALU.add,
             )
 
-        def clamp(g, j):
+        def clamp(g, j, h0=0, h1=2):
             nc.vector.tensor_scalar(
-                out=line[g][:, j, :],
-                in0=line[g][:, j, :],
+                out=line[g][:, h0:h1, j, :],
+                in0=line[g][:, h0:h1, j, :],
                 scalar1=lower[:, j : j + 1],
                 scalar2=upper[:, j : j + 1],
                 op0=ALU.max,
                 op1=ALU.min,
             )
 
-        def interleave_vector(g, t0, t1):
-            nc.vector.tensor_copy(
-                out=fq[g][:, t0:t1].rearrange("p t (c i) j -> p c j i t", i=2),
-                in_=line[g][:].rearrange("p j (c i t) -> p c j i t", i=2, t=T)[:, :, :, :, t0:t1],
+        def interleave(copy, g, half, t0, t1, m0=0, m1=HALF // T):
+            first = half * HALF // T
+            copy(
+                out=fq[g][:, t0:t1, first + m0 : first + m1].rearrange("p t (c i) j -> p c j i t", i=2),
+                in_=line[g][:, half, :, T * m0 : T * m1].rearrange("p j (c i t) -> p c j i t", i=2, t=T)[:, :, :, :, t0:t1],
             )
 
-        def interleave_scalar(g, t):
+        def interleave_tile(g, t):
             nc.scalar.copy(
-                out=fq[g][:, t].rearrange("p (c i) j -> p c j i", i=2),
-                in_=line[g][:].rearrange("p j (c i t) -> p c j i t", i=2, t=T)[:, :, :, :, t],
+                out=fq[g][:, t].rearrange("p (a c i) j -> p a c j i", a=2, i=2),
+                in_=line[g][:].rearrange("p a j (c i t) -> p a c j i t", i=2, t=T)[:, :, :, :, :, t],
             )
+
+        def finish(g, h, c0=0, c1=T * E, engine=nc.sync):
+            apply_gate(g, h, c0, c1)
+            store(g, h, c0, c1, engine)
 
         def quantize(g, t0=0, t1=T):
             nc.vector.quantize_mx(
@@ -147,7 +168,7 @@ def tile_rows_read_relu1_gate_kernel(tc, q, qa, S, og, out):
         def multiply(g):
             for k in range(H // PAIR):
                 for t in range(T):
-                    for h in range(PAIR * k, PAIR * (k + 1)):
+                    for h in reversed(range(PAIR * k, PAIR * (k + 1))):
                         rows = slice(ROWS * h, ROWS * (h + 1))
                         nc.tensor.matmul_mx(
                             out=banks[g, h][:, t, :],
@@ -159,19 +180,19 @@ def tile_rows_read_relu1_gate_kernel(tc, q, qa, S, og, out):
                             stop=True,
                         )
 
-        def sigmoid(g, h):
-            nc.scalar.activation(out=sig[g, h][:], in_=gate[g, h], func=ACT.Sigmoid)
+        def sigmoid(g, h, c0=0, c1=T * E):
+            nc.scalar.activation(out=sig[g, h][:, c0:c1], in_=gate[g, h][:, c0:c1], func=ACT.Sigmoid)
 
-        def apply_gate(g, h):
+        def apply_gate(g, h, c0=0, c1=T * E):
             nc.vector.tensor_tensor(
-                out=res[g, h][:],
-                in0=banks[g, h][:].rearrange("p t e -> p (t e)"),
-                in1=sig[g, h][:],
+                out=res[g, h][:, c0:c1],
+                in0=banks[g, h][:].rearrange("p t e -> p (t e)")[:, c0:c1],
+                in1=sig[g, h][:, c0:c1],
                 op=ALU.mult,
             )
 
-        def store(g, h, engine=nc.sync):
-            engine.dma_start(out=out_v[g, :, h, :], in_=res[g, h][:])
+        def store(g, h, c0=0, c1=T * E, engine=nc.sync):
+            engine.dma_start(out=out_v[g, :, h, c0:c1], in_=res[g, h][:, c0:c1])
 
         load_weight(nc.scalar, 0)
         load_weight(nc.scalar, 1)
@@ -189,39 +210,46 @@ def tile_rows_read_relu1_gate_kernel(tc, q, qa, S, og, out):
         load_gate(1, 0, 2)
         load_gate(1, 2, 3)
         load_gate(1, 3, 4)
+        on_vector, on_scalar = nc.vector.tensor_copy, nc.scalar.copy
         bounds()
         weigh_scalar(0, 0)
         weigh_vector(0, 1)
         clamp(0, 1)
-        weigh_scalar(0, 2)
+        weigh_scalar(0, 2, 0, 1)
+        weigh_scalar(0, 2, 1, 2)
         weigh_vector(0, 3)
         clamp(0, 0)
         clamp(0, 3)
-        clamp(0, 2)
-        round_state()
-        interleave_scalar(0, 3)
-        interleave_vector(0, 0, 3)
+        clamp(0, 2, 0, 1)
+        clamp(0, 2, 1, 2)
+        round_state(on_scalar)
+        interleave(on_vector, 0, 0, 0, 3)
+        interleave(on_vector, 0, 1, 0, 3)
+        interleave_tile(0, 3)
         quantize_state()
         quantize(0)
         multiply(0)
         weigh_scalar(1, 0)
         weigh_scalar(1, 1)
-        weigh_scalar(1, 2)
-        weigh_vector(1, 3)
         clamp(1, 0)
+        weigh_scalar(1, 2, 0, 1)
+        weigh_scalar(1, 2, 1, 2)
+        weigh_vector(1, 3)
         clamp(1, 1)
         clamp(1, 3)
-        clamp(1, 2)
+        clamp(1, 2, 0, 1)
+        clamp(1, 2, 1, 2)
         sigmoid(0, 0)
-        interleave_scalar(1, 3)
-        interleave_vector(1, 0, 3)
-        apply_gate(0, 0)
-        store(0, 0)
-        quantize(1)
+        sigmoid(0, 1)
+        interleave(on_vector, 1, 0, 0, 2)
+        interleave(on_vector, 1, 1, 0, 2)
+        interleave_tile(1, 2)
+        interleave_tile(1, 3)
+        finish(0, 0)
+        quantize(1, 0, 2)
+        finish(0, 1)
+        quantize(1, 2, 4)
         multiply(1)
-        for g in range(GROUPS):
-            for h in range(H):
-                if (g, h) != (0, 0):
-                    sigmoid(g, h)
-                    apply_gate(g, h)
-                    store(g, h)
+        for g, h in [(g, h) for g in range(GROUPS) for h in range(H)][2:]:
+            sigmoid(g, h)
+            finish(g, h)

@@ -58,8 +58,8 @@ def tile_rows_read_relu1_gate_kernel(tc, q, qa, S, og, out):
                 sig[g, h] = sb.tile([P, T * E], F32, name="sig%d_%d" % (g, h))
                 res[g, h] = sb.tile([P, T * E], F32, name="res%d_%d" % (g, h))
 
-        def load_weight(engine, h):
-            engine.dma_start(out=weight[ROWS * h : ROWS * (h + 1), :], in_=qa_v)
+        def load_weight():
+            nc.scalar.dma_start(out=weight[:], in_=qa_v.partition_broadcast(H))
 
         def warm_up():
             warm_in = sb.tile([P, 1], F32, name="warm_in")
@@ -194,12 +194,9 @@ def tile_rows_read_relu1_gate_kernel(tc, q, qa, S, og, out):
         def store(g, h, c0=0, c1=T * E, engine=nc.sync):
             engine.dma_start(out=out_v[g, :, h, c0:c1], in_=res[g, h][:, c0:c1])
 
-        load_weight(nc.scalar, 0)
-        load_weight(nc.scalar, 1)
+        load_weight()
         warm_up()
         load_q(0, 0, 2)
-        load_weight(nc.sync, 2)
-        load_weight(nc.sync, 3)
         load_q(0, 2, 4)
         load_state()
         load_q(1, 0, 2)

@@ -58,8 +58,8 @@ def tile_rows_read_relu1_gate_kernel(tc, q, qa, S, og, out):
                 sig[g, h] = sb.tile([P, T * E], F32, name="sig%d_%d" % (g, h))
                 res[g, h] = sb.tile([P, T * E], F32, name="res%d_%d" % (g, h))
 
-        def load_weight():
-            nc.scalar.dma_start(out=weight[:], in_=qa_v.partition_broadcast(H))
+        def load_weight(engine, h):
+            engine.dma_start(out=weight[ROWS * h : ROWS * (h + 1), :], in_=qa_v)
 
         def warm_up():
             warm_in = sb.tile([P, 1], F32, name="warm_in")
@@ -67,9 +67,11 @@ def tile_rows_read_relu1_gate_kernel(tc, q, qa, S, og, out):
             nc.vector.memset(warm_in[:], 0.0)
             nc.scalar.activation(out=warm_out[:], in_=warm_in[:], func=ACT.Sigmoid)
 
-        def bounds():
-            nc.vector.tensor_scalar_mul(out=base[:], in0=weight[:], scalar1=OFFSET)
+        def sign_and_base():
             nc.vector.tensor_scalar(out=side[:], in0=weight[:], scalar1=0.0, scalar2=0.5, op0=ALU.is_ge, op1=ALU.subtract)
+            nc.vector.tensor_scalar_mul(out=base[:], in0=weight[:], scalar1=OFFSET)
+
+        def bounds():
             nc.vector.scalar_tensor_tensor(out=lower[:], in0=side[:], scalar=FAR, in1=base[:], op0=ALU.mult, op1=ALU.min)
             nc.vector.scalar_tensor_tensor(out=upper[:], in0=side[:], scalar=FAR, in1=base[:], op0=ALU.mult, op1=ALU.max)
 
@@ -95,10 +97,16 @@ def tile_rows_read_relu1_gate_kernel(tc, q, qa, S, og, out):
             nc.sync.dma_start(out=s_raw[:], in_=s_v)
 
         def load_gate(g, h0, h1, engine=nc.sync):
-            tile = sb.tile([P, h1 - h0, T * E], F32, name="gate%d_%d" % (g, h0))
-            engine.dma_start(out=tile[:], in_=og_v[g, :, h0:h1, :])
+            tile = sb.tile([P, (h1 - h0) * T * E], F32, name="gate%d_%d" % (g, h0), align_bytes=64)
+            engine.dma_start(out=tile[:].rearrange("p (h c) -> p h c", h=h1 - h0), in_=og_v[g, :, h0:h1, :])
             for h in range(h0, h1):
-                gate[g, h] = tile[:, h - h0, :]
+                gate[g, h] = tile[:, (h - h0) * T * E : (h - h0 + 1) * T * E]
+
+        def grouped(g, t0, t1):
+            if g == 1 and t0 >= PAIR:
+                late = gate[0, 0].bitcast(BF16).rearrange("p (t m j) -> p t m j", t=PAIR, j=PACK)
+                return late[:, t0 - PAIR : t1 - PAIR]
+            return fq[g][:, t0:t1]
 
         def round_state(copy):
             copy(
@@ -125,10 +133,10 @@ def tile_rows_read_relu1_gate_kernel(tc, q, qa, S, og, out):
             nc.vector.tensor_scalar(
                 out=line[g][:, h0:h1, j, :],
                 in0=source(g, j, h0, h1),
-                scalar1=weight[:, j : j + 1],
-                scalar2=base[:, j : j + 1],
-                op0=ALU.mult,
-                op1=ALU.add,
+                scalar1=OFFSET,
+                scalar2=weight[:, j : j + 1],
+                op0=ALU.add,
+                op1=ALU.mult,
             )
 
         def clamp(g, j, h0=0, h1=2):
@@ -150,8 +158,18 @@ def tile_rows_read_relu1_gate_kernel(tc, q, qa, S, og, out):
 
         def interleave_tile(g, t):
             nc.scalar.copy(
-                out=fq[g][:, t].rearrange("p (a c i) j -> p a c j i", a=2, i=2),
+                out=grouped(g, t, t + 1)[:, 0].rearrange("p (a c i) j -> p a c j i", a=2, i=2),
                 in_=line[g][:].rearrange("p a j (c i t) -> p a c j i t", i=2, t=T)[:, :, :, :, :, t],
+            )
+
+        def interleave_gpsimd(g, t):
+            nc.gpsimd.tensor_scalar(
+                out=grouped(g, t, t + 1)[:, 0].rearrange("p (a m) j -> p a m j", a=2),
+                in0=line[g][:].rearrange("p a j (m t) -> p a m j t", t=T)[:, :, :, :, t],
+                scalar1=1.0,
+                scalar2=0.0,
+                op0=ALU.mult,
+                op1=ALU.add,
             )
 
         def finish(g, h, c0=0, c1=T * E, engine=nc.sync):
@@ -162,13 +180,13 @@ def tile_rows_read_relu1_gate_kernel(tc, q, qa, S, og, out):
             nc.vector.quantize_mx(
                 out=q_codes[g][:, t0:t1].rearrange("p t m -> p (t m)").bitcast(FP8X4),
                 scales=q_scales[g][:, t0:t1].rearrange("p t m -> p (t m)"),
-                in_=fq[g][:, t0:t1].rearrange("p t m j -> p (t m j)"),
+                in_=grouped(g, t0, t1).rearrange("p t m j -> p (t m j)"),
             )
 
-        def multiply(g):
-            for k in range(H // PAIR):
-                for t in range(T):
-                    for h in reversed(range(PAIR * k, PAIR * (k + 1))):
+        def multiply(g, order=range(T), together=PAIR):
+            for k in range(H // together):
+                for t in order:
+                    for h in reversed(range(together * k, together * (k + 1))):
                         rows = slice(ROWS * h, ROWS * (h + 1))
                         nc.tensor.matmul_mx(
                             out=banks[g, h][:, t, :],
@@ -194,9 +212,12 @@ def tile_rows_read_relu1_gate_kernel(tc, q, qa, S, og, out):
         def store(g, h, c0=0, c1=T * E, engine=nc.sync):
             engine.dma_start(out=out_v[g, :, h, c0:c1], in_=res[g, h][:, c0:c1])
 
-        load_weight()
+        load_weight(nc.scalar, 0)
+        load_weight(nc.scalar, 1)
         warm_up()
         load_q(0, 0, 2)
+        load_weight(nc.sync, 2)
+        load_weight(nc.sync, 3)
         load_q(0, 2, 4)
         load_state()
         load_q(1, 0, 2)
@@ -208,17 +229,20 @@ def tile_rows_read_relu1_gate_kernel(tc, q, qa, S, og, out):
         load_gate(1, 2, 3)
         load_gate(1, 3, 4)
         on_vector, on_scalar = nc.vector.tensor_copy, nc.scalar.copy
-        bounds()
+        sign_and_base()
         weigh_scalar(0, 0)
         weigh_vector(0, 1)
+        bounds()
         clamp(0, 1)
+        clamp(0, 0)
         weigh_scalar(0, 2, 0, 1)
         weigh_scalar(0, 2, 1, 2)
-        weigh_vector(0, 3)
-        clamp(0, 0)
-        clamp(0, 3)
+        weigh_vector(0, 3, 0, 1)
+        weigh_vector(0, 3, 1, 2)
         clamp(0, 2, 0, 1)
+        clamp(0, 3, 0, 1)
         clamp(0, 2, 1, 2)
+        clamp(0, 3, 1, 2)
         round_state(on_scalar)
         interleave(on_vector, 0, 0, 0, 3)
         interleave(on_vector, 0, 1, 0, 3)
@@ -229,24 +253,26 @@ def tile_rows_read_relu1_gate_kernel(tc, q, qa, S, og, out):
         weigh_scalar(1, 0)
         weigh_scalar(1, 1)
         clamp(1, 0)
+        clamp(1, 1)
         weigh_scalar(1, 2, 0, 1)
         weigh_scalar(1, 2, 1, 2)
-        weigh_vector(1, 3)
-        clamp(1, 1)
-        clamp(1, 3)
+        weigh_vector(1, 3, 0, 1)
+        weigh_vector(1, 3, 1, 2)
         clamp(1, 2, 0, 1)
+        clamp(1, 3, 0, 1)
         clamp(1, 2, 1, 2)
+        clamp(1, 3, 1, 2)
         sigmoid(0, 0)
         sigmoid(0, 1)
         interleave(on_vector, 1, 0, 0, 2)
-        interleave(on_vector, 1, 1, 0, 2)
+        interleave_gpsimd(1, 3)
         interleave_tile(1, 2)
-        interleave_tile(1, 3)
         finish(0, 0)
-        quantize(1, 0, 2)
         finish(0, 1)
+        interleave(on_vector, 1, 1, 0, 2)
         quantize(1, 2, 4)
-        multiply(1)
+        quantize(1, 0, 2)
+        multiply(1, (2, 3, 0, 1), H)
         for g, h in [(g, h) for g in range(GROUPS) for h in range(H)][2:]:
             sigmoid(g, h)
             finish(g, h)

@@ -156,6 +156,13 @@ def tile_rows_read_relu1_gate_kernel(tc, q, qa, S, og, out):
                 in_=line[g][:, half, :, T * m0 : T * m1].rearrange("p j (c i t) -> p c j i t", i=2, t=T)[:, :, :, :, t0:t1],
             )
 
+        def interleave_one(copy, g, half, t):
+            first = half * HALF // T
+            copy(
+                out=fq[g][:, t, first : first + HALF // T].rearrange("p (c i) j -> p c j i", i=2),
+                in_=line[g][:, half].rearrange("p j (c i t) -> p c j i t", i=2, t=T)[:, :, :, :, t],
+            )
+
         def interleave_tile(g, t):
             nc.scalar.copy(
                 out=grouped(g, t, t + 1)[:, 0].rearrange("p (a c i) j -> p a c j i", a=2, i=2),
@@ -224,7 +231,8 @@ def tile_rows_read_relu1_gate_kernel(tc, q, qa, S, og, out):
         load_q(1, 2, 4)
         load_gate(0, 0, 1)
         load_gate(0, 1, 2)
-        load_gate(0, 2, 4)
+        load_gate(0, 2, 3)
+        load_gate(0, 3, 4)
         load_gate(1, 0, 2)
         load_gate(1, 2, 3)
         load_gate(1, 3, 4)
@@ -267,12 +275,14 @@ def tile_rows_read_relu1_gate_kernel(tc, q, qa, S, og, out):
         interleave(on_vector, 1, 0, 0, 2)
         interleave_gpsimd(1, 3)
         interleave_tile(1, 2)
+        interleave_one(on_scalar, 1, 1, 1)
         finish(0, 0)
         finish(0, 1)
-        interleave(on_vector, 1, 1, 0, 2)
+        interleave_one(on_vector, 1, 1, 0)
         quantize(1, 2, 4)
+        multiply(1, (2, 3), H)
         quantize(1, 0, 2)
-        multiply(1, (2, 3, 0, 1), H)
+        multiply(1, (0, 1), PAIR)
         for g, h in [(g, h) for g in range(GROUPS) for h in range(H)][2:]:
             sigmoid(g, h)
             finish(g, h)

@@ -23,6 +23,7 @@ HALF = GROUP // 2
 PAIR = 2
 OFFSET = 0.125
 FAR = 3.0e38
+LATE = 2
 
 
 def tile_rows_read_relu1_gate_kernel(tc, q, qa, S, og, out):
@@ -53,10 +54,10 @@ def tile_rows_read_relu1_gate_kernel(tc, q, qa, S, og, out):
             fq[g] = sb.tile([P, T, P, PACK], BF16, name="fq%d" % g, align_bytes=64)
             q_codes[g] = sb.tile([P, T, P], U32, name="q_codes%d" % g, align_bytes=64)
             q_scales[g] = sb.tile([P, T, P], U8, name="q_scales%d" % g, align_bytes=64)
+            res[g] = sb.tile([P, H, T * E], F32, name="res%d" % g)
             for h in range(H):
                 banks[g, h] = ps.tile([P, T, E], F32, name="y%d_%d" % (g, h))
                 sig[g, h] = sb.tile([P, T * E], F32, name="sig%d_%d" % (g, h))
-                res[g, h] = sb.tile([P, T * E], F32, name="res%d_%d" % (g, h))
 
         def load_weight(engine, h):
             engine.dma_start(out=weight[ROWS * h : ROWS * (h + 1), :], in_=qa_v)
@@ -67,8 +68,10 @@ def tile_rows_read_relu1_gate_kernel(tc, q, qa, S, og, out):
             nc.vector.memset(warm_in[:], 0.0)
             nc.scalar.activation(out=warm_out[:], in_=warm_in[:], func=ACT.Sigmoid)
 
-        def sign_and_base():
+        def make_side():
             nc.vector.tensor_scalar(out=side[:], in0=weight[:], scalar1=0.0, scalar2=0.5, op0=ALU.is_ge, op1=ALU.subtract)
+
+        def make_base():
             nc.vector.tensor_scalar_mul(out=base[:], in0=weight[:], scalar1=OFFSET)
 
         def bounds():
@@ -81,29 +84,17 @@ def tile_rows_read_relu1_gate_kernel(tc, q, qa, S, og, out):
             for j in range(j0, j1):
                 q_raw[g, j] = tile[:, j - j0, :]
 
-        def load_cols(g, half):
-            tile = sb.tile([P, PACK, HALF], F32, name="q_cols%d_%d" % (g, half))
-            n0 = GROUP * g + HALF * half
-            nc.sync.dma_start(out=tile[:], in_=q_v[:, :, n0 : n0 + HALF])
-            for j in range(PACK):
-                q_raw[g, j, half] = tile[:, j : j + 1, :]
-
-        def source(g, j, h0, h1):
-            if (g, j, h0) in q_raw:
-                return q_raw[g, j, h0]
-            return halves(q_raw[g, j], h0, h1)
-
         def load_state():
             nc.sync.dma_start(out=s_raw[:], in_=s_v)
 
-        def load_gate(g, h0, h1, engine=nc.sync):
+        def load_gate(g, h0, h1):
             tile = sb.tile([P, (h1 - h0) * T * E], F32, name="gate%d_%d" % (g, h0), align_bytes=64)
-            engine.dma_start(out=tile[:].rearrange("p (h c) -> p h c", h=h1 - h0), in_=og_v[g, :, h0:h1, :])
+            nc.sync.dma_start(out=tile[:].rearrange("p (h c) -> p h c", h=h1 - h0), in_=og_v[g, :, h0:h1, :])
             for h in range(h0, h1):
                 gate[g, h] = tile[:, (h - h0) * T * E : (h - h0 + 1) * T * E]
 
         def grouped(g, t0, t1):
-            if g == 1 and t0 >= PAIR:
+            if g == 1 and t0 >= LATE:
                 late = gate[0, 0].bitcast(BF16).rearrange("p (t m j) -> p t m j", t=PAIR, j=PACK)
                 return late[:, t0 - PAIR : t1 - PAIR]
             return fq[g][:, t0:t1]
@@ -123,7 +114,7 @@ def tile_rows_read_relu1_gate_kernel(tc, q, qa, S, og, out):
         def weigh_scalar(g, j, h0=0, h1=2):
             nc.scalar.activation(
                 out=line[g][:, h0:h1, j, :],
-                in_=source(g, j, h0, h1),
+                in_=halves(q_raw[g, j], h0, h1),
                 func=ACT.Identity,
                 scale=weight[:, j : j + 1],
                 bias=base[:, j : j + 1],
@@ -132,7 +123,7 @@ def tile_rows_read_relu1_gate_kernel(tc, q, qa, S, og, out):
         def weigh_vector(g, j, h0=0, h1=2):
             nc.vector.tensor_scalar(
                 out=line[g][:, h0:h1, j, :],
-                in0=source(g, j, h0, h1),
+                in0=halves(q_raw[g, j], h0, h1),
                 scalar1=OFFSET,
                 scalar2=weight[:, j : j + 1],
                 op0=ALU.add,
@@ -149,17 +140,17 @@ def tile_rows_read_relu1_gate_kernel(tc, q, qa, S, og, out):
                 op1=ALU.min,
             )
 
-        def interleave(copy, g, half, t0, t1, m0=0, m1=HALF // T):
+        def interleave(copy, g, half, t0, t1):
             first = half * HALF // T
             copy(
-                out=fq[g][:, t0:t1, first + m0 : first + m1].rearrange("p t (c i) j -> p c j i t", i=2),
-                in_=line[g][:, half, :, T * m0 : T * m1].rearrange("p j (c i t) -> p c j i t", i=2, t=T)[:, :, :, :, t0:t1],
+                out=fq[g][:, t0:t1, first : first + HALF // T].rearrange("p t (c i) j -> p c j i t", i=2),
+                in_=line[g][:, half].rearrange("p j (c i t) -> p c j i t", i=2, t=T)[:, :, :, :, t0:t1],
             )
 
         def interleave_one(copy, g, half, t):
             first = half * HALF // T
             copy(
-                out=fq[g][:, t, first : first + HALF // T].rearrange("p (c i) j -> p c j i", i=2),
+                out=grouped(g, t, t + 1)[:, 0, first : first + HALF // T].rearrange("p (c i) j -> p c j i", i=2),
                 in_=line[g][:, half].rearrange("p j (c i t) -> p c j i t", i=2, t=T)[:, :, :, :, t],
             )
 
@@ -178,10 +169,6 @@ def tile_rows_read_relu1_gate_kernel(tc, q, qa, S, og, out):
                 op0=ALU.mult,
                 op1=ALU.add,
             )
-
-        def finish(g, h, c0=0, c1=T * E, engine=nc.sync):
-            apply_gate(g, h, c0, c1)
-            store(g, h, c0, c1, engine)
 
         def quantize(g, t0=0, t1=T):
             nc.vector.quantize_mx(
@@ -205,20 +192,25 @@ def tile_rows_read_relu1_gate_kernel(tc, q, qa, S, og, out):
                             stop=True,
                         )
 
-        def sigmoid(g, h, c0=0, c1=T * E):
-            nc.scalar.activation(out=sig[g, h][:, c0:c1], in_=gate[g, h][:, c0:c1], func=ACT.Sigmoid)
+        def sigmoid(g, h):
+            nc.scalar.activation(out=sig[g, h][:], in_=gate[g, h], func=ACT.Sigmoid)
 
-        def apply_gate(g, h, c0=0, c1=T * E):
+        def apply_gate(g, h):
             nc.vector.tensor_tensor(
-                out=res[g, h][:, c0:c1],
-                in0=banks[g, h][:].rearrange("p t e -> p (t e)")[:, c0:c1],
-                in1=sig[g, h][:, c0:c1],
+                out=res[g][:, h, :],
+                in0=banks[g, h][:].rearrange("p t e -> p (t e)"),
+                in1=sig[g, h][:],
                 op=ALU.mult,
             )
 
-        def store(g, h, c0=0, c1=T * E, engine=nc.sync):
-            engine.dma_start(out=out_v[g, :, h, c0:c1], in_=res[g, h][:, c0:c1])
+        def store(g, h0, h1):
+            nc.sync.dma_start(out=out_v[g, :, h0:h1, :], in_=res[g][:, h0:h1, :])
 
+        def finish(g, h):
+            apply_gate(g, h)
+            store(g, h, h + 1)
+
+        on_vector, on_scalar = nc.vector.tensor_copy, nc.scalar.copy
         load_weight(nc.scalar, 0)
         load_weight(nc.scalar, 1)
         warm_up()
@@ -236,53 +228,52 @@ def tile_rows_read_relu1_gate_kernel(tc, q, qa, S, og, out):
         load_gate(1, 0, 2)
         load_gate(1, 2, 3)
         load_gate(1, 3, 4)
-        on_vector, on_scalar = nc.vector.tensor_copy, nc.scalar.copy
-        sign_and_base()
-        weigh_scalar(0, 0)
+        make_base()
+        make_side()
         weigh_vector(0, 1)
+        weigh_scalar(0, 0)
         bounds()
-        clamp(0, 1)
-        clamp(0, 0)
         weigh_scalar(0, 2, 0, 1)
         weigh_scalar(0, 2, 1, 2)
+        clamp(0, 1)
         weigh_vector(0, 3, 0, 1)
         weigh_vector(0, 3, 1, 2)
-        clamp(0, 2, 0, 1)
+        clamp(0, 0)
         clamp(0, 3, 0, 1)
-        clamp(0, 2, 1, 2)
+        clamp(0, 2, 0, 1)
         clamp(0, 3, 1, 2)
+        clamp(0, 2, 1, 2)
         round_state(on_scalar)
         interleave(on_vector, 0, 0, 0, 3)
         interleave(on_vector, 0, 1, 0, 3)
         interleave_tile(0, 3)
+        weigh_scalar(1, 0)
+        weigh_scalar(1, 1)
         quantize_state()
         quantize(0)
         multiply(0)
-        weigh_scalar(1, 0)
-        weigh_scalar(1, 1)
         clamp(1, 0)
-        clamp(1, 1)
         weigh_scalar(1, 2, 0, 1)
         weigh_scalar(1, 2, 1, 2)
         weigh_vector(1, 3, 0, 1)
         weigh_vector(1, 3, 1, 2)
-        clamp(1, 2, 0, 1)
+        clamp(1, 1)
         clamp(1, 3, 0, 1)
-        clamp(1, 2, 1, 2)
+        clamp(1, 2, 0, 1)
         clamp(1, 3, 1, 2)
+        clamp(1, 2, 1, 2)
+        interleave(on_vector, 1, 0, 0, 2)
+        interleave(on_vector, 1, 1, 0, 2)
         sigmoid(0, 0)
         sigmoid(0, 1)
-        interleave(on_vector, 1, 0, 0, 2)
         interleave_gpsimd(1, 3)
         interleave_tile(1, 2)
-        interleave_one(on_scalar, 1, 1, 1)
         finish(0, 0)
         finish(0, 1)
-        interleave_one(on_vector, 1, 1, 0)
-        quantize(1, 2, 4)
-        multiply(1, (2, 3), H)
         quantize(1, 0, 2)
-        multiply(1, (0, 1), PAIR)
+        multiply(1, (0, 1), H)
+        quantize(1, 2, 4)
+        multiply(1, (2, 3), PAIR)
         for g, h in [(g, h) for g in range(GROUPS) for h in range(H)][2:]:
             sigmoid(g, h)
             finish(g, h)

@@ -262,18 +262,19 @@ def tile_rows_read_relu1_gate_kernel(tc, q, qa, S, og, out):
         clamp(1, 2, 0, 1)
         clamp(1, 3, 1, 2)
         clamp(1, 2, 1, 2)
-        interleave(on_vector, 1, 0, 0, 2)
-        interleave(on_vector, 1, 1, 0, 2)
         sigmoid(0, 0)
         sigmoid(0, 1)
+        interleave(on_vector, 1, 0, 0, 2)
         interleave_gpsimd(1, 3)
         interleave_tile(1, 2)
+        interleave_one(on_scalar, 1, 1, 1)
         finish(0, 0)
         finish(0, 1)
-        quantize(1, 0, 2)
-        multiply(1, (0, 1), H)
+        interleave_one(on_vector, 1, 1, 0)
         quantize(1, 2, 4)
-        multiply(1, (2, 3), PAIR)
+        multiply(1, (2, 3), H)
+        quantize(1, 0, 2)
+        multiply(1, (0, 1), PAIR)
         for g, h in [(g, h) for g in range(GROUPS) for h in range(H)][2:]:
             sigmoid(g, h)
             finish(g, h)

@@ -44,7 +44,7 @@ def tile_rows_read_relu1_gate_kernel(tc, q, qa, S, og, out):
         side = sb.tile([P, PACK], F32, name="side")
         lower = sb.tile([P, PACK], BF16, name="lower")
         upper = sb.tile([P, PACK], BF16, name="upper")
-        s_raw = sb.tile([P, PACK, E], F32, name="s_raw")
+        s_raw = sb.tile([P, PACK, E], F32, name="s_raw", align_bytes=256)
         s_bf = sb.tile([P, E, PACK], BF16, name="s_bf", align_bytes=64)
         s_codes = sb.tile([P, E], U32, name="s_codes", align_bytes=64)
         s_scales = sb.tile([P, E], U8, name="s_scales", align_bytes=64)
@@ -54,7 +54,7 @@ def tile_rows_read_relu1_gate_kernel(tc, q, qa, S, og, out):
             fq[g] = sb.tile([P, T, P, PACK], BF16, name="fq%d" % g, align_bytes=64)
             q_codes[g] = sb.tile([P, T, P], U32, name="q_codes%d" % g, align_bytes=64)
             q_scales[g] = sb.tile([P, T, P], U8, name="q_scales%d" % g, align_bytes=64)
-            res[g] = sb.tile([P, H, T * E], F32, name="res%d" % g)
+            res[g] = sb.tile([P, H, T * E], F32, name="res%d" % g, align_bytes=256)
             for h in range(H):
                 banks[g, h] = ps.tile([P, T, E], F32, name="y%d_%d" % (g, h))
                 sig[g, h] = sb.tile([P, T * E], F32, name="sig%d_%d" % (g, h))
@@ -79,7 +79,7 @@ def tile_rows_read_relu1_gate_kernel(tc, q, qa, S, og, out):
             nc.vector.scalar_tensor_tensor(out=upper[:], in0=side[:], scalar=FAR, in1=base[:], op0=ALU.mult, op1=ALU.max)
 
         def load_q(g, j0, j1):
-            tile = sb.tile([P, j1 - j0, GROUP], F32, name="q_raw%d_%d" % (g, j0))
+            tile = sb.tile([P, j1 - j0, GROUP], F32, name="q_raw%d_%d" % (g, j0), align_bytes=256)
             nc.sync.dma_start(out=tile[:], in_=q_v[:, j0:j1, GROUP * g : GROUP * (g + 1)])
             for j in range(j0, j1):
                 q_raw[g, j] = tile[:, j - j0, :]
@@ -88,7 +88,7 @@ def tile_rows_read_relu1_gate_kernel(tc, q, qa, S, og, out):
             nc.sync.dma_start(out=s_raw[:], in_=s_v)
 
         def load_gate(g, h0, h1):
-            tile = sb.tile([P, (h1 - h0) * T * E], F32, name="gate%d_%d" % (g, h0), align_bytes=64)
+            tile = sb.tile([P, (h1 - h0) * T * E], F32, name="gate%d_%d" % (g, h0), align_bytes=256)
             nc.sync.dma_start(out=tile[:].rearrange("p (h c) -> p h c", h=h1 - h0), in_=og_v[g, :, h0:h1, :])
             for h in range(h0, h1):
                 gate[g, h] = tile[:, (h - h0) * T * E : (h - h0 + 1) * T * E]

@@ -96,7 +96,7 @@ def tile_rows_read_relu1_gate_kernel(tc, q, qa, S, og, out):
         def grouped(g, t0, t1):
             if g == 1 and t0 >= LATE:
                 late = gate[0, 0].bitcast(BF16).rearrange("p (t m j) -> p t m j", t=PAIR, j=PACK)
-                return late[:, t0 - PAIR : t1 - PAIR]
+                return late[:, t0 - LATE : t1 - LATE]
             return fq[g][:, t0:t1]
 
         def round_state(copy):
@@ -177,20 +177,25 @@ def tile_rows_read_relu1_gate_kernel(tc, q, qa, S, og, out):
                 in_=grouped(g, t0, t1).rearrange("p t m j -> p (t m j)"),
             )
 
-        def multiply(g, order=range(T), together=PAIR):
-            for k in range(H // together):
-                for t in order:
-                    for h in reversed(range(together * k, together * (k + 1))):
-                        rows = slice(ROWS * h, ROWS * (h + 1))
-                        nc.tensor.matmul_mx(
-                            out=banks[g, h][:, t, :],
-                            lhsT=q_codes[g][rows, t, :].bitcast(FP8X4),
-                            lhsT_scale=q_scales[g][rows, t, :],
-                            rhs=s_codes[rows, :].bitcast(FP8X4),
-                            rhs_scale=s_scales[rows, :],
-                            start=True,
-                            stop=True,
-                        )
+        def calls(tiles):
+            rest = [(h, t) for t in tiles for h in (3, 2)]
+            order = []
+            for k, t in enumerate(tiles):
+                order.extend([(1, t), (0, t), rest[k]])
+            return order + rest[len(tiles) :]
+
+        def multiply(g, order):
+            for h, t in order:
+                rows = slice(ROWS * h, ROWS * (h + 1))
+                nc.tensor.matmul_mx(
+                    out=banks[g, h][:, t, :],
+                    lhsT=q_codes[g][rows, t, :].bitcast(FP8X4),
+                    lhsT_scale=q_scales[g][rows, t, :],
+                    rhs=s_codes[rows, :].bitcast(FP8X4),
+                    rhs_scale=s_scales[rows, :],
+                    start=True,
+                    stop=True,
+                )
 
         def sigmoid(g, h):
             nc.scalar.activation(out=sig[g, h][:], in_=gate[g, h], func=ACT.Sigmoid)
@@ -250,8 +255,11 @@ def tile_rows_read_relu1_gate_kernel(tc, q, qa, S, og, out):
         weigh_scalar(1, 0)
         weigh_scalar(1, 1)
         quantize_state()
-        quantize(0)
-        multiply(0)
+        first = calls((0, 1, 2, 3))
+        quantize(0, 0, 2)
+        multiply(0, first[:6])
+        quantize(0, 2, 4)
+        multiply(0, first[6:])
         clamp(1, 0)
         weigh_scalar(1, 2, 0, 1)
         weigh_scalar(1, 2, 1, 2)
@@ -272,9 +280,10 @@ def tile_rows_read_relu1_gate_kernel(tc, q, qa, S, og, out):
         finish(0, 1)
         interleave_one(on_vector, 1, 1, 0)
         quantize(1, 2, 4)
-        multiply(1, (2, 3), H)
+        second = calls((2, 3, 0, 1))
+        multiply(1, second[:6])
         quantize(1, 0, 2)
-        multiply(1, (0, 1), PAIR)
+        multiply(1, second[6:])
         for g, h in [(g, h) for g in range(GROUPS) for h in range(H)][2:]:
             sigmoid(g, h)
             finish(g, h)

from contextlib import ExitStack

import concourse.mybir as mybir

H, D, N, E = 4, 128, 1024, 128
FLOPS = 2 * H * N * D * E

F32 = mybir.dt.float32
BF16 = mybir.dt.bfloat16
U32 = mybir.dt.uint32
U8 = mybir.dt.uint8
FP8X4 = mybir.dt.float8_e4m3fn_x4
ACT = mybir.ActivationFunctionType
ALU = mybir.AluOpType

P = 128
PACK = 4
ROWS = D // PACK
T = 4
GROUP = P * T
GROUPS = N // GROUP
HALF = GROUP // 2
PAIR = 2
OFFSET = 0.125
FAR = 3.0e38
LATE = 2


def tile_rows_read_relu1_gate_kernel(tc, q, qa, S, og, out):
    nc = tc.nc
    q_v = q.rearrange("h (p j) n -> (h p) j n", j=PACK)
    s_v = S.rearrange("h (p j) e -> (h p) j e", j=PACK)
    qa_v = qa.rearrange("(p j) o -> p (j o)", j=PACK)
    og_v = og.rearrange("h (g m t) e -> g m h (t e)", g=GROUPS, t=T)
    out_v = out.rearrange("h (g m t) e -> g m h (t e)", g=GROUPS, t=T)

    with ExitStack() as ctx:
        sb = ctx.enter_context(tc.tile_pool(name="sb", bufs=1))
        ps = ctx.enter_context(tc.psum_pool(name="ps", bufs=1))
        ctx.enter_context(tc.manual_schedule())

        weight = sb.tile([P, PACK], F32, name="weight")
        base = sb.tile([P, PACK], F32, name="base")
        side = sb.tile([P, PACK], F32, name="side")
        lower = sb.tile([P, PACK], BF16, name="lower")
        upper = sb.tile([P, PACK], BF16, name="upper")
        s_raw = sb.tile([P, PACK, E], F32, name="s_raw", align_bytes=256)
        s_bf = sb.tile([P, E, PACK], BF16, name="s_bf", align_bytes=64)
        s_codes = sb.tile([P, E], U32, name="s_codes", align_bytes=64)
        s_scales = sb.tile([P, E], U8, name="s_scales", align_bytes=64)
        q_raw, gate, line, fq, q_codes, q_scales, banks, res, sig = {}, {}, {}, {}, {}, {}, {}, {}, {}
        for g in range(GROUPS):
            line[g] = sb.tile([P, 2, PACK, HALF], BF16, name="line%d" % g, align_bytes=64)
            fq[g] = sb.tile([P, T, P, PACK], BF16, name="fq%d" % g, align_bytes=64)
            q_codes[g] = sb.tile([P, T, P], U32, name="q_codes%d" % g, align_bytes=64)
            q_scales[g] = sb.tile([P, T, P], U8, name="q_scales%d" % g, align_bytes=64)
            res[g] = sb.tile([P, H, T * E], F32, name="res%d" % g, align_bytes=256)
            for h in range(H):
                banks[g, h] = ps.tile([P, T, E], F32, name="y%d_%d" % (g, h))
                sig[g, h] = sb.tile([P, T * E], F32, name="sig%d_%d" % (g, h))

        def load_weight(engine, h):
            engine.dma_start(out=weight[ROWS * h : ROWS * (h + 1), :], in_=qa_v)

        def warm_up():
            warm_in = sb.tile([P, 1], F32, name="warm_in")
            warm_out = sb.tile([P, 1], F32, name="warm_out")
            nc.vector.memset(warm_in[:], 0.0)
            nc.scalar.activation(out=warm_out[:], in_=warm_in[:], func=ACT.Sigmoid)

        def make_side():
            nc.vector.tensor_scalar(out=side[:], in0=weight[:], scalar1=0.0, scalar2=0.5, op0=ALU.is_ge, op1=ALU.subtract)

        def make_base():
            nc.vector.tensor_scalar_mul(out=base[:], in0=weight[:], scalar1=OFFSET)

        def bounds():
            nc.vector.scalar_tensor_tensor(out=lower[:], in0=side[:], scalar=FAR, in1=base[:], op0=ALU.mult, op1=ALU.min)
            nc.vector.scalar_tensor_tensor(out=upper[:], in0=side[:], scalar=FAR, in1=base[:], op0=ALU.mult, op1=ALU.max)

        def load_q(g, j0, j1):
            tile = sb.tile([P, j1 - j0, GROUP], F32, name="q_raw%d_%d" % (g, j0), align_bytes=256)
            nc.sync.dma_start(out=tile[:], in_=q_v[:, j0:j1, GROUP * g : GROUP * (g + 1)])
            for j in range(j0, j1):
                q_raw[g, j] = tile[:, j - j0, :]

        def load_state():
            nc.sync.dma_start(out=s_raw[:], in_=s_v)

        def load_gate(g, h0, h1):
            tile = sb.tile([P, (h1 - h0) * T * E], F32, name="gate%d_%d" % (g, h0), align_bytes=256)
            nc.sync.dma_start(out=tile[:].rearrange("p (h c) -> p h c", h=h1 - h0), in_=og_v[g, :, h0:h1, :])
            for h in range(h0, h1):
                gate[g, h] = tile[:, (h - h0) * T * E : (h - h0 + 1) * T * E]

        def grouped(g, t0, t1):
            if g == 1 and t0 >= LATE:
                late = gate[0, 0].bitcast(BF16).rearrange("p (t m j) -> p t m j", t=PAIR, j=PACK)
                return late[:, t0 - LATE : t1 - LATE]
            return fq[g][:, t0:t1]

        def round_state(copy):
            copy(
                out=s_bf[:].rearrange("p (c i) j -> p c j i", i=4),
                in_=s_raw[:].rearrange("p j (c i) -> p c j i", i=4),
            )

        def quantize_state():
            nc.vector.quantize_mx(out=s_codes[:].bitcast(FP8X4), scales=s_scales[:], in_=s_bf[:].rearrange("p e j -> p (e j)"))

        def halves(row, h0, h1):
            return row.rearrange("p (a n) -> p a n", a=2)[:, h0:h1, :]

        def weigh_scalar(g, j, h0=0, h1=2):
            nc.scalar.activation(
                out=line[g][:, h0:h1, j, :],
                in_=halves(q_raw[g, j], h0, h1),
                func=ACT.Identity,
                scale=weight[:, j : j + 1],
                bias=base[:, j : j + 1],
            )

        def weigh_vector(g, j, h0=0, h1=2):
            nc.vector.tensor_scalar(
                out=line[g][:, h0:h1, j, :],
                in0=halves(q_raw[g, j], h0, h1),
                scalar1=OFFSET,
                scalar2=weight[:, j : j + 1],
                op0=ALU.add,
                op1=ALU.mult,
            )

        def clamp(g, j, h0=0, h1=2):
            nc.vector.tensor_scalar(
                out=line[g][:, h0:h1, j, :],
                in0=line[g][:, h0:h1, j, :],
                scalar1=lower[:, j : j + 1],
                scalar2=upper[:, j : j + 1],
                op0=ALU.max,
                op1=ALU.min,
            )

        def interleave(copy, g, half, t0, t1):
            first = half * HALF // T
            copy(
                out=fq[g][:, t0:t1, first : first + HALF // T].rearrange("p t (c i) j -> p c j i t", i=2),
                in_=line[g][:, half].rearrange("p j (c i t) -> p c j i t", i=2, t=T)[:, :, :, :, t0:t1],
            )

        def interleave_one(copy, g, half, t):
            first = half * HALF // T
            copy(
                out=grouped(g, t, t + 1)[:, 0, first : first + HALF // T].rearrange("p (c i) j -> p c j i", i=2),
                in_=line[g][:, half].rearrange("p j (c i t) -> p c j i t", i=2, t=T)[:, :, :, :, t],
            )

        def interleave_tile(g, t):
            nc.scalar.copy(
                out=grouped(g, t, t + 1)[:, 0].rearrange("p (a c i) j -> p a c j i", a=2, i=2),
                in_=line[g][:].rearrange("p a j (c i t) -> p a c j i t", i=2, t=T)[:, :, :, :, :, t],
            )

        def interleave_gpsimd(g, t):
            nc.gpsimd.tensor_scalar(
                out=grouped(g, t, t + 1)[:, 0].rearrange("p (a m) j -> p a m j", a=2),
                in0=line[g][:].rearrange("p a j (m t) -> p a m j t", t=T)[:, :, :, :, t],
                scalar1=1.0,
                scalar2=0.0,
                op0=ALU.mult,
                op1=ALU.add,
            )

        def quantize(g, t0=0, t1=T):
            nc.vector.quantize_mx(
                out=q_codes[g][:, t0:t1].rearrange("p t m -> p (t m)").bitcast(FP8X4),
                scales=q_scales[g][:, t0:t1].rearrange("p t m -> p (t m)"),
                in_=grouped(g, t0, t1).rearrange("p t m j -> p (t m j)"),
            )

        def calls(tiles):
            rest = [(h, t) for t in tiles for h in (3, 2)]
            order = []
            for k, t in enumerate(tiles):
                order.extend([(1, t), (0, t), rest[k]])
            return order + rest[len(tiles) :]

        def multiply(g, order):
            for h, t in order:
                rows = slice(ROWS * h, ROWS * (h + 1))
                nc.tensor.matmul_mx(
                    out=banks[g, h][:, t, :],
                    lhsT=q_codes[g][rows, t, :].bitcast(FP8X4),
                    lhsT_scale=q_scales[g][rows, t, :],
                    rhs=s_codes[rows, :].bitcast(FP8X4),
                    rhs_scale=s_scales[rows, :],
                    start=True,
                    stop=True,
                )

        def sigmoid(g, h):
            nc.scalar.activation(out=sig[g, h][:], in_=gate[g, h], func=ACT.Sigmoid)

        def apply_gate(g, h):
            nc.vector.tensor_tensor(
                out=res[g][:, h, :],
                in0=banks[g, h][:].rearrange("p t e -> p (t e)"),
                in1=sig[g, h][:],
                op=ALU.mult,
            )

        def store(g, h0, h1):
            nc.sync.dma_start(out=out_v[g, :, h0:h1, :], in_=res[g][:, h0:h1, :])

        def finish(g, h):
            apply_gate(g, h)
            store(g, h, h + 1)

        on_vector, on_scalar = nc.vector.tensor_copy, nc.scalar.copy
        load_weight(nc.scalar, 0)
        load_weight(nc.scalar, 1)
        warm_up()
        load_q(0, 0, 2)
        load_weight(nc.sync, 2)
        load_weight(nc.sync, 3)
        load_q(0, 2, 4)
        load_state()
        load_q(1, 0, 2)
        load_q(1, 2, 4)
        load_gate(0, 0, 1)
        load_gate(0, 1, 2)
        load_gate(0, 2, 3)
        load_gate(0, 3, 4)
        load_gate(1, 0, 2)
        load_gate(1, 2, 3)
        load_gate(1, 3, 4)
        make_base()
        make_side()
        weigh_vector(0, 1)
        weigh_scalar(0, 0)
        bounds()
        weigh_scalar(0, 2, 0, 1)
        weigh_scalar(0, 2, 1, 2)
        clamp(0, 1)
        weigh_vector(0, 3, 0, 1)
        weigh_vector(0, 3, 1, 2)
        clamp(0, 0)
        clamp(0, 3, 0, 1)
        clamp(0, 2, 0, 1)
        clamp(0, 3, 1, 2)
        clamp(0, 2, 1, 2)
        round_state(on_scalar)
        interleave(on_vector, 0, 0, 0, 3)
        interleave(on_vector, 0, 1, 0, 3)
        interleave_tile(0, 3)
        weigh_scalar(1, 0)
        weigh_scalar(1, 1)
        quantize_state()
        first = calls((0, 1, 2, 3))
        quantize(0, 0, 2)
        multiply(0, first[:6])
        quantize(0, 2, 4)
        multiply(0, first[6:])
        clamp(1, 0)
        weigh_scalar(1, 2, 0, 1)
        weigh_scalar(1, 2, 1, 2)
        weigh_vector(1, 3, 0, 1)
        weigh_vector(1, 3, 1, 2)
        clamp(1, 1)
        clamp(1, 3, 0, 1)
        clamp(1, 2, 0, 1)
        clamp(1, 3, 1, 2)
        clamp(1, 2, 1, 2)
        sigmoid(0, 0)
        sigmoid(0, 1)
        interleave(on_vector, 1, 0, 0, 2)
        interleave_gpsimd(1, 3)
        interleave_tile(1, 2)
        interleave_one(on_scalar, 1, 1, 1)
        finish(0, 0)
        finish(0, 1)
        interleave_one(on_vector, 1, 1, 0)
        quantize(1, 2, 4)
        second = calls((2, 3, 0, 1))
        multiply(1, second[:6])
        quantize(1, 0, 2)
        multiply(1, second[6:])
        for g, h in [(g, h) for g in range(GROUPS) for h in range(H)][2:]:
            sigmoid(g, h)
            finish(g, h)
